import numpy as np, ml_dtypes
CORES = [6,15,38,47]
N = 4
import mx_ref
BF = ml_dtypes.bfloat16
def cols(t, e):
    v = np.concatenate([t.reshape(128, -1, 4), np.zeros((128, 1, 4), BF)], axis=1)
    return np.ascontiguousarray(v[:, e]).reshape(128, -1)
def cut(t, i, w=512):
    return t[:, w * i:w * i + w]
def f(rng, *shape):
    return mx_ref.flush((rng.standard_normal(shape, dtype=np.float32) * np.exp2(rng.integers(-2, 3, shape[:-1] + (1,)))).astype(BF))
def wide(rng, *shape, cols=0):
    v = rng.standard_normal(shape, dtype=np.float32) * np.exp2(rng.integers(-12, 13, shape)).astype(np.float32)
    if cols: v *= np.repeat(np.exp2(rng.integers(-cols, cols + 1, shape[:-2] + (1, shape[-1] // 4))) * (rng.random(shape[:-2] + (1, shape[-1] // 4)) > 0.0625), 4, axis=-1).astype(np.float32)
    return mx_ref.flush(v.astype(BF))
P, K, R, O = 256, 64, 6, 2
PART = [1, 2, 1, 2, 1, 2]
def scores(c, qt):
    k = mx_ref.quantize(np.concatenate([qt[r][:, :4 * R] for r in range(N)], axis=1))
    s = [mx_ref.matmul(mx_ref.quantize(cut(c[q], i)), k) for q in range(N) for i in range(P // 128)]
    return np.concatenate(s).reshape(N * P, N, R)
def play(s):
    held, use, out = np.arange(N * P).reshape(N, P), np.zeros((N, P), np.float32), []
    for t in range(R):
        left = []
        for r in range(N):
            v = s[held[r], r, t]
            use[r] = use[r] + v * v
            left.append(np.argsort(use[r], kind="stable")[:K])
        new = held.copy()
        for r in range(N):
            p = r ^ PART[t]
            new[r, left[r]] = held[p, left[p]]
            use[r, left[r]] = 0
        held = new
        out.append(held)
    return np.stack(out)
def fit(s):
    a = np.abs(s)
    return bool(np.isfinite(a).all() and ((a == 0) | (a >= 2.0 ** -60) & (a <= 2.0 ** 60)).all())
def times(t, v):
    return mx_ref.flush((t.astype(np.float32) * np.asarray(v, np.float32)).astype(BF))
def plain(rng):
    q = np.array(f(rng, N, 128, 512))
    q[:, :, 4 * R:] = 0
    return {"c": f(rng, N, 128, 4 * P), "qt": q, "w": f(rng, N, 128, 512 * O)}
def first(make, good=None):
    for i in range(50):
        d = make()
        s = scores(d["c"], d["qt"])
        if fit(s) and (good is None or good(s)): return d
    raise RuntimeError("no draw of 50 is fit")
def athome(s):
    h, a = play(s), np.ones((N, R + 1, P), bool)
    for r in range(N):
        for t in range(R): a[r, t + 1] = np.isin(np.arange(P * r, P * r + P), h[t, r])
    return a
def setup_inputs(rng):
    return first(lambda: plain(rng))
def setup_inputs_sides(rng):
    top = np.arange(128) < 64
    def make():
        d = plain(rng)
        half = np.stack([rng.permutation(P) < P // 2 for r in range(N)])
        d["c"] = times(d["c"], np.repeat(half[:, None, :] == top[None, :, None], 4, axis=2))
        for t in range(R):
            g = np.where(top == (PART[t] == 1), 1.0, 2.0 ** -6) * 4.0 ** t
            d["qt"][:, :, 4 * t:4 * t + 4] = times(d["qt"][:, :, 4 * t:4 * t + 4], g[None, :, None])
        return d
    def good(s):
        a = athome(s)
        return bool((~a[:, :-1] & a[:, 1:]).any(axis=(1, 2)).all())
    return first(make, good)
def setup_inputs_ties(rng):
    def make():
        d = plain(rng)
        d["c"] = np.stack([times(cols(d["c"][r], rng.integers(0, 6, P)), np.repeat(1 - 2 * rng.integers(0, 2, P), 4)) for r in range(N)])
        return d
    def good(s):
        for r in range(N):
            v = s[P * r:P * r + P, r, 0]
            u = np.sort(v * v)
            if u[K - 1] != u[K]: return False
        return True
    return first(make, good)
def setup_inputs_shrink(rng):
    low = np.arange(N) >= N - N // 4
    def make():
        d = plain(rng)
        size = np.exp2(np.where(low, -30.0, 23.0)[:, None] + 2 * rng.random((N, P))) * (1 - 2 * rng.integers(0, 2, (N, P)))
        d["c"] = ((1 + rng.random((N, 128, 4 * P))) * np.repeat(size, 4, axis=1)[:, None, :]).astype(np.float32).astype(BF)
        on = ~low[:, None] | np.stack([rng.permutation(128) < 2 for r in range(N)])
        for t in range(R):
            g = np.exp2(np.where(low, 8.0 * (R - 1 - t) - 30.0, 21.0 - 8.0 * t))
            d["qt"][:, :, 4 * t:4 * t + 4] = ((1 + rng.random((N, 128, 4))) * (g[:, None] * on)[:, :, None]).astype(np.float32).astype(BF)
        return d
    def good(s):
        h, a, b = play(s), np.zeros(N, bool), np.zeros(N, bool)
        for r in range(N):
            at, use, since = np.arange(P * r, P * r + P), np.zeros(P, np.float32), np.zeros(P, int)
            if low[r] and np.abs(s[at, r, R - 1]).max() > 2.0 ** -50 or not low[r] and np.abs(s[at, r, 0]).min() < 2.0 ** 50: return False
            for t in range(R):
                v = s[at, r]
                use = use + v[:, t] * v[:, t]
                sums = np.concatenate([np.zeros((P, 1), np.float32), np.cumsum(v * v, axis=1)], axis=1)
                diff = sums[:, t + 1] - sums[np.arange(P), since]
                a[r] |= (np.argsort(use, kind="stable")[:K] != np.argsort(diff, kind="stable")[:K]).any()
                b[r] |= np.sort(use)[K - 1] > 1e30
                moved = h[t, r] != at
                at = h[t, r]
                use[moved] = 0
                since[moved] = t + 1
        return bool(2 * a.sum() > N and 2 * b.sum() > N)
    return first(make, good)
def setup_inputs_turn(rng):
    on = (np.arange(128) // (128 // N))[None, :] == np.arange(N)[:, None]
    def make():
        d = plain(rng)
        d["c"] = times(d["c"], np.where(on, 2.0 ** -8, 1.0)[:, :, None])
        d["qt"] = times(d["qt"], on[:, :, None])
        return d
    return first(make, lambda s: bool((~athome(s)).any(axis=1).all()))
def setup_inputs_spread(rng):
    return first(lambda: {**plain(rng), "c": wide(rng, N, 128, 4 * P, cols=6)})
def check_inputs(d):
    b = []
    for k in ("c", "qt", "w"):
        v = np.abs(d[k].astype(np.float32))
        if not (np.isfinite(v).all() and ((v == 0) | (v >= 2.0 ** -30) & (v <= 2.0 ** 30)).all()): b.append("a value of " + k)
    if (d["qt"][:, :, 4 * R:].astype(np.float32) != 0).any(): b.append("qt has numbers behind its first R columns")
    if not b and not fit(scores(d["c"], d["qt"])): b.append("a score")
    return b
def reference(c, qt, w):
    held = play(scores(c, qt))
    every = np.concatenate([c[q] for q in range(N)], axis=1)
    y = np.zeros((N, 128, R * O * P), np.float32)
    for r in range(N):
        u, at = np.unique(held[:, r].reshape(-1), return_inverse=True)
        at = at.reshape(R, P)
        q = mx_ref.quantize(cols(every, np.concatenate([u, np.full(-len(u) % 4, -1)])))
        for o in range(O):
            z = mx_ref.matmul(mx_ref.quantize(cut(w[r], o)), q)
            for t in range(R):
                i = (t * O + o) * P
                y[r, :, i:i + P] = z[:, at[t]]
    return {"y": y}

@@ -1,0 +1,350 @@
+from concourse.mybir import dt, AluOpType, ActivationFunctionType
+
+P, K, R, O = 256, 64, 6, 2
+PART = [1, 2, 1, 2, 1, 2]
+W = P + K
+CODE, PLANE = "float8_e4m3fn_x4", "uint8"
+
+SCRATCH = {
+    "cin": ("sbuf", [128, 4 * P], "bfloat16"),
+    "qin": ("sbuf", [128, 512], "bfloat16"),
+    "win": ("sbuf", [128, 512 * O], "bfloat16"),
+    "qk": ("sbuf", [128, 128], CODE), "qks": ("sbuf", [128, 128], PLANE),
+    "qr": ("sbuf", [128, 128 * R], CODE), "qrs": ("sbuf", [128, 128 * R], PLANE),
+    "wk": ("sbuf", [128, 128 * O], CODE), "wks": ("sbuf", [128, 128 * O], PLANE),
+    "far": ("sbuf", [128, P], CODE), "fars": ("sbuf", [128, P], PLANE),
+    "offq": ("sbuf", [128, 8 * R], "uint16"),
+    "lst": ("sbuf", [128, R * K // 16], "uint16"),
+    "lland": ("sbuf", [128, K // 16], "uint16"),
+    "mrg": ("sbuf", [128, R * P // 16], "uint16"),
+    "U": ("sbuf", [128, R * P], "float32"),
+    "sqn": ("sbuf", [128, P], "float32"),
+    "sqa": ("sbuf", [128, K], "float32"),
+    "uc": ("sbuf", [128, 2], "float32"),
+    "us": ("sbuf", [128, 2], "float32"),
+    "X": ("sbuf", [128, 832], "bfloat16"),
+    "G": ("sbuf", [128, 832], "bfloat16"),
+    "SO": ("sbuf", [128, 832], "bfloat16"),
+    "RT": ("sbuf", [128, 64], "bfloat16"),
+    "RB": ("sbuf", [128, P], "bfloat16"),
+    "ne1": ("sbuf", [128, 512], "bfloat16"),
+    "lo1": ("sbuf", [128, 512], "bfloat16"),
+    "tab1": ("sbuf", [128, 512], "bfloat16"),
+    "ne2": ("sbuf", [128, 520], "bfloat16"),
+    "lo2": ("sbuf", [128, 520], "bfloat16"),
+    "tab2": ("sbuf", [128, 520], "bfloat16"),
+    "du": ("sbuf", [128, 512], "bfloat16"),
+    "du2": ("sbuf", [128, 512], "bfloat16"),
+    "dl": ("sbuf", [128, 16], "uint16"),
+    "ma": ("sbuf", [128, 16], "float32"),
+    "mb": ("sbuf", [128, 16], "float32"),
+    "mc": ("sbuf", [128, 16], "float32"),
+    "md": ("sbuf", [128, 16], "float32"),
+    "fc": ("sbuf", [128, 16], "float32"),
+    "tg": ("sbuf", [128, 4], "bfloat16"),
+    "i16": ("sbuf", [128, 16], "int32"),
+    "ip": ("sbuf", [128, 1], "int32"),
+    "ipm": ("sbuf", [128, 1], "int32"),
+    "idf": ("sbuf", [128, 1], "float32"),
+    "yw": ("sbuf", [128, (R + 1) * O * W], "float32"),
+    "pc": ("psum", [128, 1024], "float32"),
+    "pa": ("psum", [128, 512], "float32"),
+    "pr": ("psum", [128, 512], "float32"),
+    "py": ("psum", [128, 512 * O], "float32"),
+}
+SEMAPHORES = ["sv", "ss", "sp", "sg", "ldc", "ldq", "ldw", "loc", "sty", "arl"]
+for _t in range(R):
+    for _n, _w in (("H", P), ("M", W), ("S", K)):
+        SCRATCH["%s%d" % (_n, _t)] = ("sbuf", [128, _w], CODE)
+        SCRATCH["%s%ds" % (_n, _t)] = ("sbuf", [128, _w], PLANE)
+    SEMAPHORES += [_n + str(_t) for _n in ("cp", "arc", "ars")]
+
+
+def rank_program(g, core, T, topo):
+    rank = T.rank_of(core)
+    if rank is None:
+        return
+    A, F = AluOpType, ActivationFunctionType
+    vec, act, ten, syn = g.vector, g.scalar, g.tensor, g.sync
+    queue = {"v": vec, "s": act, "p": ten, "g": g, "y": syn}
+    count = {"v": 0, "s": 0, "p": 0, "g": 0}
+    own = {"v": "sv", "s": "ss", "p": "sp", "g": "sg"}
+    seen = {}
+    sent = [0]
+
+    def wait(q, *deps):
+        top = {}
+        for d in deps:
+            if d is not None:
+                top[d[0]] = max(top.get(d[0], 0), d[1])
+        for s in top:
+            if seen.get((q, s), 0) < top[s]:
+                queue[q].wait_ge(T.sem[s], top[s])
+                seen[(q, s)] = top[s]
+
+    def done(q, ins):
+        count[q] += 1
+        ins.then_inc(T.sem[own[q]], 1)
+        return (own[q], count[q])
+
+    def send(out_ap, in_ap, sem, t):
+        dst = T.cores[rank ^ PART[t]]
+        rid, pid = topo.addr(dst)[:2]
+        g.remote_dma(out_ap=out_ap, in_ap=in_ap, remote_sem=T.sem[sem], local_sem=T.sem["loc"], pid=pid, routing_id=rid, dma_engine_mask=topo.mask(core, dst))
+        sent[0] += len(topo.engines(core, dst))
+
+    def came(sem, t):
+        return (sem, len(topo.engines(T.cores[rank ^ PART[t]], core)))
+
+    def u8(v):
+        return v.bitcast(dt.uint8)
+
+    def pick(out, win, a, b, c, d, off, deps):
+        wait("v", *deps)
+        return done("v", vec.tensor_copy(T[out][:, a:b].bitcast(dt.uint32), T[win][:, c:d].bitcast(dt.uint32).indirect(off)))
+
+    def picks(out, win, a, b, c, d, off, deps):
+        wait("s", *deps)
+        return done("s", act.activation(T[out + "s"][:, a:b], T[win + "s"][:, c:d].indirect(off), F.Copy))
+
+    def mm(out, n, st, a, mv, b, deps):
+        wait("p", *deps)
+        return done("p", ten.matmul_mx(out, T[st][:, a:a + 128], T[st + "s"][:, a:a + 128], T[mv][:, b:b + n], T[mv + "s"][:, b:b + n], True, True))
+
+    def fill(ap, x, *deps):
+        wait("v", *deps)
+        return done("v", vec.memset(ap, x))
+
+    def ts(out, in0, s1, s2, op0, op1, *deps):
+        wait("v", *deps)
+        if op1 is None:
+            return done("v", vec.tensor_scalar(out, in0, s1, None, op0))
+        return done("v", vec.tensor_scalar(out, in0, s1, s2, op0, op1))
+
+    def tt(out, in0, in1, op, *deps):
+        wait("v", *deps)
+        return done("v", vec.tensor_tensor(out, in0, in1, op))
+
+    def scan(out, d0, d1, op0, op1, *deps):
+        wait("v", *deps)
+        return done("v", vec.tensor_tensor_scan(out, d0, d1, 0.0, op0, op1))
+
+    def turn(out, in_, *deps):
+        wait("v", *deps)
+        return done("v", vec.transpose(out, in_))
+
+    def copy(out, in_, *deps):
+        wait("v", *deps)
+        return done("v", vec.tensor_copy(out, in_))
+
+    def func(out, in_, f, *deps):
+        wait("s", *deps)
+        return done("s", act.activation(out, in_, f))
+
+    act.dma_start(T.qin[:], T.qt[:]).then_inc(T.sem.ldq, 16)
+    syn.dma_start(T.cin[:], T.c[:]).then_inc(T.sem.ldc, 16)
+    syn.dma_start(T.win[:], T.w[:]).then_inc(T.sem.ldw, 16)
+    toff = [fill(T.offq[:, 0:8], 0)]
+    tg1 = fill(T.G[:], 1.0)
+    ti1 = done("g", g.iota(T.ip[:], [[1, 1]], 0, 1))
+    ti2 = done("g", g.iota(T.i16[:], [[16, 16]], 0, 1))
+    wait("g", tg1)
+    tk = None
+    for h in range(2):
+        v = T.G[:, 416 * h:416 * h + 128]
+        tk = done("g", g.affine_select(v, v, [[-1, 128]], A.not_equal, 0.0, 0, 1))
+    for h in range(2):
+        fill(T.G[:, 416 * h + 128:416 * h + 129], -1.0, tg1)
+        fill(T.X[:, 416 * h + 384:416 * h + 416], 0.0)
+        tcon = fill(T.SO[:, 416 * h + 384:416 * h + 416], 0.0)
+    ta = ts(T.ipm[:], T.ip[:], 15, None, A.bitwise_and, None, ti1)
+    ta = tt(T.idf[:], T.ip[:], T.ipm[:], A.subtract, ta)
+    fill(T.tab1[:], 1.0)
+    tfc = ts(T.fc[:], T.i16[:], T.idf[:], None, A.subtract, None, ta, ti2)
+    fill(T.tab2[:], 1.0)
+    for i in range(2):
+        tdl = copy(T.dl[:, i:16:2], T.fc[:, 0:8], tfc)
+
+    wait("v", ("ldq", 16))
+    tq = done("v", vec.quantize_mx(T.qk[:], T.qks[:], T.qin[:]))
+    trc, trs = [None] * R, [None] * R
+
+    def query(t, *deps):
+        off = T.offq[:, 8 * t:8 * t + 8]
+        trc[t] = pick("qr", "qk", 128 * t, 128 * t + 128, 0, 128, off, deps)
+        trs[t] = picks("qr", "qk", 128 * t, 128 * t + 128, 0, 128, off, deps)
+
+    query(0, tq, toff[0])
+    wait("v", ("ldc", 16))
+    x = done("v", vec.quantize_mx(T.H0[:], T.H0s[:], T.cin[:]))
+    hc = hs = [x, x]
+
+    wait("g", x)
+    send(u8(T.far[:]), u8(T.H0[:]), "arc0", 0)
+    send(T.fars[:], T.H0s[:], "ars0", 0)
+
+    t0 = mm(T.pr[:, 0:P], P, "qr", 0, "H0", 0, (trc[0], trs[0], x))
+    tu = func(T.U[:, 0:P], T.pr[:, 0:P], F.Square, t0)
+    ttg = copy(T.tg[:], T.fc[:, 0:4])
+    fill(T.ne2[:, 0:520:130], 0.0)
+    ttab = fill(T.ne2[:, 1:520:130], 1.0)
+    toff += [fill(T.offq[:, 8 * i:8 * i + 8], i) for i in (1, 2)]
+    wait("v", ("ldw", 16))
+    tw = done("v", vec.quantize_mx(T.wk[:], T.wks[:], T.win[:]))
+
+    tsqa = tm = tadd = tus = None
+    tv = [None, None]
+    tyc = [None, None]
+    tyw = [None, None]
+    tsq = tu
+    arr = [(came("arc%d" % t, t), came("ars%d" % t, t)) for t in range(R)]
+
+    def products(t, tm):
+        z = [mm(T.py[:, 512 * o:512 * o + 128], 128, "wk", 128 * o, "M%d" % t, W - 128, (tw, arr[t][0], arr[t][1], ("cp%d" % t, 32), tyc[o])) for o in range(O)]
+        tail = t == R - 1
+        for o in range(O):
+            b = (t * O + o) * W
+            src = T.py[:, 512 * o + 128 - K:512 * o + 128]
+            z[o] = copy(T.yw[:, b + P:b + W], src, z[o]) if tail else z[o]
+        for o in range(O):
+            b = (t * O + o) * W
+            n = ((t + 1) * O + o) * W
+            src = T.py[:, 512 * o + 128 - K:512 * o + 128]
+            win = T.yw[:, b:b + W].indirect(T.mrg[:, 16 * t:16 * t + 16])
+            x = z[o]
+            if not tail:
+                tyc[o] = x = func(T.yw[:, b + P:b + W], src, F.Copy, x)
+            if tail and o == 0:
+                x = copy(T.yw[:, n:n + P], win, x, tyw[o], tm)
+            else:
+                x = func(T.yw[:, n:n + P], win, F.Copy, x, tyw[o], tm)
+            tyw[o] = x
+            q = "s" if tail and o == 1 else "y"
+            wait(q, x)
+            queue[q].dma_start(T.y[:, (t * O + o) * P:(t * O + o) * P + P], T.yw[:, n:n + P]).then_inc(T.sem.sty, 16)
+
+    def ahead(t, *deps):
+        x = mm(T.pr[:, 0:P], P, "qr", 128 * t, "H%d" % (t - 1), 0, (trc[t], trs[t], tsq))
+        return func(T.sqn[:], T.pr[:, 0:P], F.Square, x, *deps)
+
+    for t in range(R):
+        H, M, S = "H%d" % t, "M%d" % t, "S%d" % t
+        last = t == R - 1
+        u = t * P
+        tc = [mm(T.pc[:, 512 * h:512 * h + 128], 128, H, 128 * h, "qk", 0, (hc[h], hs[h], tq, tv[h])) for h in range(2)]
+        a = P - K if last else 0
+        wait("y", hc[1], hs[1])
+        syn.dma_start(u8(T[M][:, a:P]), u8(T[H][:, a:P])).then_inc(T.sem["cp%d" % t], 16)
+        syn.dma_start(T[M + "s"][:, a:P], T[H + "s"][:, a:P]).then_inc(T.sem["cp%d" % t], 16)
+        if t > 1 and not last:
+            tsq = ahead(t + 1, tadd)
+        if t == 1:
+            for o in range(O):
+                z = mm(T.py[:, 512 * o:512 * o + P], P, "wk", 128 * o, "H0", 0, (tw,))
+                tyw[o] = tyc[o] = func(T.yw[:, o * W:o * W + P], T.py[:, 512 * o:512 * o + P], F.Copy, z)
+        if t:
+            products(t - 1, tm)
+        tb = []
+        uses = [T.uc[:, h:h + 1] for h in range(2)]
+
+        def use(h):
+            s = T.pc[:, 512 * h + t:512 * h + t + 1]
+            if t:
+                tv[h] = ts(uses[h], s, s, T.us[:, h:h + 1], A.mult, A.add, tc[h], tus_old)
+            else:
+                tv[h] = ts(uses[h], s, s, None, A.mult, None, tc[h])
+
+        def equal(h):
+            return ts(T.X[:, 416 * h:416 * h + 128], T.U[:, u + 128 * h:u + 128 * h + 128], uses[h], None, A.is_equal, None, tv[h], tu)
+
+        def add_up(h, tx):
+            x = 416 * h
+            return scan(T.SO[:, x:x + 385], T.G[:, x:x + 385], T.X[:, x:x + 385], A.mult, A.add, tx, tk, tcon)
+
+        def spread(h, to):
+            tr = turn(T.RT[:, 32 * h:32 * h + 32], T.SO[:, 416 * h + 384:416 * h + 416], to)
+            wait("g", tr)
+            for a in range(4):
+                tb.append(done("g", g.partition_broadcast(T.RB[:, 128 * h + 32 * a:128 * h + 32 * a + 32], T.RT[32 * a:32 * a + 1, 32 * h:32 * h + 32], 128)))
+
+        def keep(h, to):
+            return ts(T.us[:, h:h + 1], T.SO[:, 416 * h + 384:416 * h + 385], float(K), uses[h], A.is_ge, A.mult, to)
+
+        tus_old = tus
+        use(0)
+        equal(0)
+        ts(T.X[:, 128:256], T.U[:, u:u + 128], uses[0], None, A.is_le, None)
+        tx = ts(T.X[:, 256:384], T.U[:, u + 128:u + 256], uses[0], None, A.is_lt, None)
+        use(1)
+        to = add_up(0, tx)
+        equal(1)
+        spread(0, to)
+        tx = ts(T.X[:, 416 + 128:416 + 384], T.U[:, u:u + 256], uses[1], None, A.is_le, None)
+        if not last:
+            keep(0, to)
+        to = add_up(1, tx)
+        spread(1, to)
+        if not last:
+            tus = keep(1, to)
+        if t == 0:
+            query(1, toff[1])
+            tsq = ahead(1)
+            trs[2] = picks("qr", "qk", 256, 384, 0, 128, T.offq[:, 16:24], (toff[2],))
+        if t == 1:
+            trc[2] = pick("qr", "qk", 256, 384, 0, 128, T.offq[:, 16:24], (toff[2],))
+        td = [func(T.du[:, 256 * h:256 * h + 256], T.RB[:, 128 * h:128 * h + 128].indirect(T.dl[:]), F.Copy, tb[4 * h + 3], tdl) for h in range(2)]
+        for c in range(4):
+            x = ts(T.ne1[:, 128 * c:128 * c + 128], T.RB[:, 0:128], T.tg[:, c:c + 1], None, A.not_equal, None, tb[3], ttg)
+        x = scan(T.lo1[:], T.tab1[:], T.ne1[:], A.add, A.mult, x, ttab)
+        z = copy(T.tab2[:, 1:520:130], T.lo1[:, 127:512:128], x)
+        x = [ts(T.ne2[:, 130 * c + 2:130 * c + 130], T.RB[:, 128:256], T.tg[:, c:c + 1], None, A.not_equal, None, tb[7]) for c in range(4)]
+        scan(T.lo2[:, 0:260], T.tab2[:, 0:260], T.ne2[:, 0:260], A.add, A.mult, x[1], z)
+        x = scan(T.lo2[:, 260:520], T.tab2[:, 260:520], T.ne2[:, 260:520], A.add, A.mult, x[3])
+        lst = T.lst[:, 4 * t:4 * t + 4]
+        tl = ts(lst, T.lo2[:, 129:520:130], -1.0, 255.0, A.mult, A.add, x)
+        if t == 0:
+            wait("g", tl)
+            send(T.lland[:], lst, "arl", t)
+        else:
+            x = pick(S, H, 0, K, 0, P, lst, (tl,))
+            z = picks(S, H, 0, K, 0, P, lst, (tl,))
+            wait("g", x)
+            send(u8(T[M][:, P:W]), u8(T[S][:]), "arc%d" % t, t)
+            wait("g", z)
+            send(T[M + "s"][:, P:W], T[S + "s"][:], "ars%d" % t, t)
+        if t == 1:
+            tsq = ahead(2, tadd)
+        x = turn(T.du2[:], T.du[:], *td)
+        ts(T.ma[:], T.du2[:, 0:512:32], float(P), None, A.add, None, x)
+        x = ts(T.mb[:], T.du2[:, 0:512:32], float(K), None, A.is_lt, None)
+        x = tt(T.mc[:], T.ma[:], T.mb[:], A.mult, x)
+        x = tt(T.md[:], T.mc[:], T.fc[:], A.max, x)
+        mrg = T.mrg[:, 16 * t:16 * t + 16]
+        tm = copy(mrg, T.md[:], x)
+        if not last:
+            tadd = tt(T.U[:, u + P:u + 2 * P], T.U[:, u:u + P], T.sqn[:], A.add, tsq, tu)
+        if t and t + 2 < R:
+            query(t + 2, fill(T.offq[:, 8 * t + 16:8 * t + 24], t + 2))
+        if t == 0:
+            z = came("arl", t)
+            arr[t] = (pick(M, "far", P, W, 0, P, T.lland[:], (z, arr[t][0])), picks(M, "far", P, W, 0, P, T.lland[:], (z, arr[t][1])))
+        if not last:
+            ac, as_ = arr[t]
+            cp = ("cp%d" % t, 32)
+            n = "H%d" % (t + 1)
+            z = mm(T.pa[:, 0:128], 128, "qr", 128 * (t + 1), M, W - 128, (ac, as_, cp, trc[t + 1], trs[t + 1], tsqa))
+            hc, hs = [], []
+            for h in range(2):
+                off = T.mrg[:, 16 * t + 8 * h:16 * t + 8 * h + 8]
+                hc.append(pick(n, M, 128 * h, 128 * h + 128, 0, W, off, (ac, cp, tm)))
+                hs.append(picks(n, M, 128 * h, 128 * h + 128, 0, W, off, (as_, cp, tm)))
+                if h == 0:
+                    tsqa = func(T.sqa[:], T.pa[:, 128 - K:128], F.Square, z, tu)
+            tu = copy(T.U[:, u + P:u + 2 * P].indirect(lst), T.sqa[:], tadd, tsqa)
+        else:
+            products(t, tm)
+
+    for q in ("v", "s", "p", "g"):
+        wait("y", (own[q], count[q]))
+    wait("y", ("sty", 16 * R * O))
+    wait("g", ("loc", sent[0]))

@@ -27,12 +27,14 @@ SCRATCH = {
     "SO": ("sbuf", [128, 832], "bfloat16"),
     "RT": ("sbuf", [128, 64], "bfloat16"),
     "RB": ("sbuf", [128, P], "bfloat16"),
-    "ne1": ("sbuf", [128, 512], "bfloat16"),
-    "lo1": ("sbuf", [128, 512], "bfloat16"),
-    "tab1": ("sbuf", [128, 512], "bfloat16"),
-    "ne2": ("sbuf", [128, 520], "bfloat16"),
-    "lo2": ("sbuf", [128, 520], "bfloat16"),
-    "tab2": ("sbuf", [128, 520], "bfloat16"),
+    "Z": ("sbuf", [128, 128], "bfloat16"),
+    "E": ("sbuf", [128, P], "bfloat16"),
+    "ET": ("sbuf", [128, P], "bfloat16"),
+    "ER": ("sbuf", [128, P], "bfloat16"),
+    "ES": ("sbuf", [128, P], "bfloat16"),
+    "fa": ("sbuf", [128, 4], "bfloat16"),
+    "fb": ("sbuf", [128, 4], "bfloat16"),
+    "pl": ("sbuf", [128, 2], "bfloat16"),
     "du": ("sbuf", [128, 512], "bfloat16"),
     "du2": ("sbuf", [128, 512], "bfloat16"),
     "dl": ("sbuf", [128, 16], "uint16"),
@@ -41,7 +43,6 @@ SCRATCH = {
     "mc": ("sbuf", [128, 16], "float32"),
     "md": ("sbuf", [128, 16], "float32"),
     "fc": ("sbuf", [128, 16], "float32"),
-    "tg": ("sbuf", [128, 4], "bfloat16"),
     "i16": ("sbuf", [128, 16], "int32"),
     "ip": ("sbuf", [128, 1], "int32"),
     "ipm": ("sbuf", [128, 1], "int32"),
@@ -148,6 +149,8 @@ def rank_program(g, core, T, topo):
     tg1 = fill(T.G[:], 1.0)
     ti1 = done("g", g.iota(T.ip[:], [[1, 1]], 0, 1))
     ti2 = done("g", g.iota(T.i16[:], [[16, 16]], 0, 1))
+    tz = done("g", g.iota(T.Z[:], [[16, 4], [0, 2], [1, 16]], 0, 0, allow_small_or_imprecise_dtypes=True))
+    tz = done("g", g.iota(T.pl[:], [[128, 2]], 0, 1, allow_small_or_imprecise_dtypes=True))
     wait("g", tg1)
     tk = None
     for h in range(2):
@@ -159,9 +162,9 @@ def rank_program(g, core, T, topo):
         tcon = fill(T.SO[:, 416 * h + 384:416 * h + 416], 0.0)
     ta = ts(T.ipm[:], T.ip[:], 15, None, A.bitwise_and, None, ti1)
     ta = tt(T.idf[:], T.ip[:], T.ipm[:], A.subtract, ta)
-    fill(T.tab1[:], 1.0)
+    ter = fill(T.ER[:], 1.0)
     tfc = ts(T.fc[:], T.i16[:], T.idf[:], None, A.subtract, None, ta, ti2)
-    fill(T.tab2[:], 1.0)
+    ter = fill(T.ER[:, 0:P:K], 0.0, ter)
     for i in range(2):
         tdl = copy(T.dl[:, i:16:2], T.fc[:, 0:8], tfc)
 
@@ -185,10 +188,8 @@ def rank_program(g, core, T, topo):
 
     t0 = mm(T.pr[:, 0:P], P, "qr", 0, "H0", 0, (trc[0], trs[0], x))
     tu = func(T.U[:, 0:P], T.pr[:, 0:P], F.Square, t0)
-    ttg = copy(T.tg[:], T.fc[:, 0:4])
-    fill(T.ne2[:, 0:520:130], 0.0)
-    ttab = fill(T.ne2[:, 1:520:130], 1.0)
     toff += [fill(T.offq[:, 8 * i:8 * i + 8], i) for i in (1, 2)]
+    query(1, toff[1])
     wait("v", ("ldw", 16))
     tw = done("v", vec.quantize_mx(T.wk[:], T.wks[:], T.win[:]))
 
@@ -270,38 +271,42 @@ def rank_program(g, core, T, topo):
         def keep(h, to):
             return ts(T.us[:, h:h + 1], T.SO[:, 416 * h + 384:416 * h + 385], float(K), uses[h], A.is_ge, A.mult, to)
 
+        def mark(h, to):
+            return ts(T.E[:, 128 * h:128 * h + 128], T.Z[:], T.SO[:, 416 * h + 384:416 * h + 385], T.pl[:, h:h + 1], A.is_equal, A.mult, to, tz)
+
+        def twice(h):
+            return func(T.du[:, 256 * h:256 * h + 256], T.RB[:, 128 * h:128 * h + 128].indirect(T.dl[:]), F.Copy, tb[4 * h + 3], tdl)
+
         tus_old = tus
         use(0)
         equal(0)
         ts(T.X[:, 128:256], T.U[:, u:u + 128], uses[0], None, A.is_le, None)
         tx = ts(T.X[:, 256:384], T.U[:, u + 128:u + 256], uses[0], None, A.is_lt, None)
         use(1)
-        to = add_up(0, tx)
+        to0 = add_up(0, tx)
         equal(1)
-        spread(0, to)
+        spread(0, to0)
         tx = ts(T.X[:, 416 + 128:416 + 384], T.U[:, u:u + 256], uses[1], None, A.is_le, None)
-        if not last:
-            keep(0, to)
+        x0 = mark(0, to0)
         to = add_up(1, tx)
-        spread(1, to)
-        if not last:
-            tus = keep(1, to)
+        turn(T.ET[:, 0:P:2], T.E[:, 0:128], x0)
         if t == 0:
-            query(1, toff[1])
             tsq = ahead(1)
             trs[2] = picks("qr", "qk", 256, 384, 0, 128, T.offq[:, 16:24], (toff[2],))
-        if t == 1:
-            trc[2] = pick("qr", "qk", 256, 384, 0, 128, T.offq[:, 16:24], (toff[2],))
-        td = [func(T.du[:, 256 * h:256 * h + 256], T.RB[:, 128 * h:128 * h + 128].indirect(T.dl[:]), F.Copy, tb[4 * h + 3], tdl) for h in range(2)]
-        for c in range(4):
-            x = ts(T.ne1[:, 128 * c:128 * c + 128], T.RB[:, 0:128], T.tg[:, c:c + 1], None, A.not_equal, None, tb[3], ttg)
-        x = scan(T.lo1[:], T.tab1[:], T.ne1[:], A.add, A.mult, x, ttab)
-        z = copy(T.tab2[:, 1:520:130], T.lo1[:, 127:512:128], x)
-        x = [ts(T.ne2[:, 130 * c + 2:130 * c + 130], T.RB[:, 128:256], T.tg[:, c:c + 1], None, A.not_equal, None, tb[7]) for c in range(4)]
-        scan(T.lo2[:, 0:260], T.tab2[:, 0:260], T.ne2[:, 0:260], A.add, A.mult, x[1], z)
-        x = scan(T.lo2[:, 260:520], T.tab2[:, 260:520], T.ne2[:, 260:520], A.add, A.mult, x[3])
+        td = [twice(0)]
+        x = mark(1, to)
+        spread(1, to)
+        x = turn(T.ET[:, 1:P:2], T.E[:, 128:256], x)
+        if not last:
+            keep(0, to0)
+        x = scan(T.ES[:], T.ER[:], T.ET[:], A.mult, A.add, x, ter)
+        if not last:
+            tus = keep(1, to)
+        x = tt(T.fa[0:64, :], T.ES[0:64, K - 1:P:K], T.ES[64:128, K - 1:P:K], A.add, x)
+        x = tt(T.fb[0:32, :], T.fa[0:32, :], T.fa[32:64, :], A.add, x)
+        for a in range(4):
+            tl = copy(T.lst[32 * a:32 * a + 32, 4 * t:4 * t + 4], T.fb[0:32, :], x)
         lst = T.lst[:, 4 * t:4 * t + 4]
-        tl = ts(lst, T.lo2[:, 129:520:130], -1.0, 255.0, A.mult, A.add, x)
         if t == 0:
             wait("g", tl)
             send(T.lland[:], lst, "arl", t)
@@ -312,7 +317,9 @@ def rank_program(g, core, T, topo):
             send(u8(T[M][:, P:W]), u8(T[S][:]), "arc%d" % t, t)
             wait("g", z)
             send(T[M + "s"][:, P:W], T[S + "s"][:], "ars%d" % t, t)
+        td.append(twice(1))
         if t == 1:
+            trc[2] = pick("qr", "qk", 256, 384, 0, 128, T.offq[:, 16:24], (toff[2],))
             tsq = ahead(2, tadd)
         x = turn(T.du2[:], T.du[:], *td)
         ts(T.ma[:], T.du2[:, 0:512:32], float(P), None, A.add, None, x)

@@ -2,7 +2,8 @@ from concourse.mybir import dt, AluOpType, ActivationFunctionType
 
 P, K, R, O = 256, 64, 6, 2
 PART = [1, 2, 1, 2, 1, 2]
-W = P + K
+W = K + P
+FAR = 1024.0
 CODE, PLANE = "float8_e4m3fn_x4", "uint8"
 
 SCRATCH = {
@@ -22,11 +23,9 @@ SCRATCH = {
     "sqa": ("sbuf", [128, K], "float32"),
     "uc": ("sbuf", [128, 2], "float32"),
     "us": ("sbuf", [128, 2], "float32"),
-    "X": ("sbuf", [128, 832], "bfloat16"),
-    "G": ("sbuf", [128, 832], "bfloat16"),
-    "SO": ("sbuf", [128, 832], "bfloat16"),
-    "RT": ("sbuf", [128, 64], "bfloat16"),
-    "RB": ("sbuf", [128, P], "bfloat16"),
+    "X": ("sbuf", [128, 768], "bfloat16"),
+    "G": ("sbuf", [128, 384], "bfloat16"),
+    "SO": ("sbuf", [128, 768], "bfloat16"),
     "Z": ("sbuf", [128, 128], "bfloat16"),
     "E": ("sbuf", [128, P], "bfloat16"),
     "ET": ("sbuf", [128, P], "bfloat16"),
@@ -35,15 +34,18 @@ SCRATCH = {
     "fa": ("sbuf", [128, 4], "bfloat16"),
     "fb": ("sbuf", [128, 4], "bfloat16"),
     "pl": ("sbuf", [128, 2], "bfloat16"),
-    "du": ("sbuf", [128, 512], "bfloat16"),
-    "du2": ("sbuf", [128, 512], "bfloat16"),
-    "dl": ("sbuf", [128, 16], "uint16"),
-    "ma": ("sbuf", [128, 16], "float32"),
-    "mb": ("sbuf", [128, 16], "float32"),
-    "mc": ("sbuf", [128, 16], "float32"),
-    "md": ("sbuf", [128, 16], "float32"),
-    "fc": ("sbuf", [128, 16], "float32"),
-    "i16": ("sbuf", [128, 16], "int32"),
+    "plk": ("sbuf", [128, 2], "float32"),
+    "st": ("sbuf", [128, 2], "float32"),
+    "sl": ("sbuf", [128, 2], "float32"),
+    "J": ("sbuf", [128, 128], "bfloat16"),
+    "JG": ("sbuf", [128, 128], "bfloat16"),
+    "Y": ("sbuf", [128, P], "bfloat16"),
+    "YT": ("sbuf", [128, P], "bfloat16"),
+    "YR": ("sbuf", [128, P], "bfloat16"),
+    "YS": ("sbuf", [128, P], "bfloat16"),
+    "ya": ("sbuf", [128, 16], "bfloat16"),
+    "yb": ("sbuf", [128, 16], "bfloat16"),
+    "iq": ("sbuf", [128, 8 * R], "int32"),
     "ip": ("sbuf", [128, 1], "int32"),
     "ipm": ("sbuf", [128, 1], "int32"),
     "idf": ("sbuf", [128, 1], "float32"),
@@ -142,42 +144,48 @@ def rank_program(g, core, T, topo):
         wait("s", *deps)
         return done("s", act.activation(out, in_, f))
 
+    def iota(out, pattern, base, step):
+        return done("g", g.iota(out, pattern, base, step, allow_small_or_imprecise_dtypes=True))
+
+    def fold(half, quarter, src, op, dep):
+        x = tt(half[0:64, :], src[0], src[1], op, dep)
+        return tt(quarter[0:32, :], half[0:32, :], half[32:64, :], op, x)
+
     act.dma_start(T.qin[:], T.qt[:]).then_inc(T.sem.ldq, 16)
     syn.dma_start(T.cin[:], T.c[:]).then_inc(T.sem.ldc, 16)
     syn.dma_start(T.win[:], T.w[:]).then_inc(T.sem.ldw, 16)
-    toff = [fill(T.offq[:, 0:8], 0)]
     tg1 = fill(T.G[:], 1.0)
-    ti1 = done("g", g.iota(T.ip[:], [[1, 1]], 0, 1))
-    ti2 = done("g", g.iota(T.i16[:], [[16, 16]], 0, 1))
-    tz = done("g", g.iota(T.Z[:], [[16, 4], [0, 2], [1, 16]], 0, 0, allow_small_or_imprecise_dtypes=True))
-    tz = done("g", g.iota(T.pl[:], [[128, 2]], 0, 1, allow_small_or_imprecise_dtypes=True))
+    tiq = done("g", g.iota(T.iq[:], [[1, R], [0, 8]], 0, 0))
+    tip = done("g", g.iota(T.ip[:], [[1, 1]], 0, 1))
     wait("g", tg1)
-    tk = None
-    for h in range(2):
-        v = T.G[:, 416 * h:416 * h + 128]
-        tk = done("g", g.affine_select(v, v, [[-1, 128]], A.not_equal, 0.0, 0, 1))
-    for h in range(2):
-        fill(T.G[:, 416 * h + 128:416 * h + 129], -1.0, tg1)
-        fill(T.X[:, 416 * h + 384:416 * h + 416], 0.0)
-        tcon = fill(T.SO[:, 416 * h + 384:416 * h + 416], 0.0)
-    ta = ts(T.ipm[:], T.ip[:], 15, None, A.bitwise_and, None, ti1)
+    tk = done("g", g.affine_select(T.G[:, 0:128], T.G[:, 0:128], [[-1, 128]], A.not_equal, 0.0, 0, 1))
+    tj = iota(T.J[:], [[32, 4], [0, 2], [1, 16]], 0, 0)
+    iota(T.Z[:], [[16, 4], [0, 2], [1, 16]], 0, 0)
+    iota(T.pl[:], [[128, 2]], 0, 1)
+    tz = iota(T.plk[:], [[128, 2]], K, 1)
+    fill(T.ER[:], 1.0)
+    ter = fill(T.YR[:], 0.0)
+    toff = copy(T.offq[:], T.iq[:], tiq)
+    ta = ts(T.ipm[:], T.ip[:], 16, None, A.bitwise_and, None, tip)
+    fill(T.G[:, 128:129], -1.0, ter)
+    fill(T.ER[:, 0:P:K], 0.0)
+    fill(T.YR[:, 0:P:16], -FAR)
     ta = tt(T.idf[:], T.ip[:], T.ipm[:], A.subtract, ta)
-    ter = fill(T.ER[:], 1.0)
-    tfc = ts(T.fc[:], T.i16[:], T.idf[:], None, A.subtract, None, ta, ti2)
-    ter = fill(T.ER[:, 0:P:K], 0.0, ter)
-    for i in range(2):
-        tdl = copy(T.dl[:, i:16:2], T.fc[:, 0:8], tfc)
 
     wait("v", ("ldq", 16))
     tq = done("v", vec.quantize_mx(T.qk[:], T.qks[:], T.qin[:]))
+    ta = ts(T.JG[:], T.J[:], T.idf[:], FAR - K, A.is_equal, A.mult, ta, tj)
     trc, trs = [None] * R, [None] * R
 
-    def query(t, *deps):
-        off = T.offq[:, 8 * t:8 * t + 8]
-        trc[t] = pick("qr", "qk", 128 * t, 128 * t + 128, 0, 128, off, deps)
-        trs[t] = picks("qr", "qk", 128 * t, 128 * t + 128, 0, 128, off, deps)
+    def query_codes(t):
+        trc[t] = pick("qr", "qk", 128 * t, 128 * t + 128, 0, 128, T.offq[:, 8 * t:8 * t + 8], (tq, toff))
 
-    query(0, tq, toff[0])
+    def query_scales(t):
+        trs[t] = picks("qr", "qk", 128 * t, 128 * t + 128, 0, 128, T.offq[:, 8 * t:8 * t + 8], (tq, toff))
+
+    query_codes(0)
+    query_scales(0)
+    query_scales(1)
     wait("v", ("ldc", 16))
     x = done("v", vec.quantize_mx(T.H0[:], T.H0s[:], T.cin[:]))
     hc = hs = [x, x]
@@ -188,33 +196,36 @@ def rank_program(g, core, T, topo):
 
     t0 = mm(T.pr[:, 0:P], P, "qr", 0, "H0", 0, (trc[0], trs[0], x))
     tu = func(T.U[:, 0:P], T.pr[:, 0:P], F.Square, t0)
-    toff += [fill(T.offq[:, 8 * i:8 * i + 8], i) for i in (1, 2)]
-    query(1, toff[1])
+    tcon = ts(T.JG[:], T.JG[:], -FAR, None, A.add, None, ta)
+    query_codes(1)
     wait("v", ("ldw", 16))
     tw = done("v", vec.quantize_mx(T.wk[:], T.wks[:], T.win[:]))
 
     tsqa = tm = tadd = tus = None
     tv = [None, None]
+    tc = [None, None]
     tyc = [None, None]
     tyw = [None, None]
     tsq = tu
     arr = [(came("arc%d" % t, t), came("ars%d" % t, t)) for t in range(R)]
+    uses = [T.uc[:, h:h + 1] for h in range(2)]
+    order = [T.SO[:, 384 * h + 383:384 * h + 384] for h in range(2)]
 
     def products(t, tm):
-        z = [mm(T.py[:, 512 * o:512 * o + 128], 128, "wk", 128 * o, "M%d" % t, W - 128, (tw, arr[t][0], arr[t][1], ("cp%d" % t, 32), tyc[o])) for o in range(O)]
+        z = [mm(T.py[:, 512 * o:512 * o + 128], 128, "wk", 128 * o, "M%d" % t, 0, (tw, arr[t][0], arr[t][1], ("cp%d" % t, 32), tyc[o])) for o in range(O)]
         tail = t == R - 1
         for o in range(O):
             b = (t * O + o) * W
-            src = T.py[:, 512 * o + 128 - K:512 * o + 128]
-            z[o] = copy(T.yw[:, b + P:b + W], src, z[o]) if tail else z[o]
+            src = T.py[:, 512 * o:512 * o + K]
+            z[o] = copy(T.yw[:, b:b + K], src, z[o]) if tail else z[o]
         for o in range(O):
             b = (t * O + o) * W
-            n = ((t + 1) * O + o) * W
-            src = T.py[:, 512 * o + 128 - K:512 * o + 128]
+            n = ((t + 1) * O + o) * W + K
+            src = T.py[:, 512 * o:512 * o + K]
             win = T.yw[:, b:b + W].indirect(T.mrg[:, 16 * t:16 * t + 16])
             x = z[o]
             if not tail:
-                tyc[o] = x = func(T.yw[:, b + P:b + W], src, F.Copy, x)
+                tyc[o] = x = func(T.yw[:, b:b + K], src, F.Copy, x)
             if tail and o == 0:
                 x = copy(T.yw[:, n:n + P], win, x, tyw[o], tm)
             else:
@@ -228,126 +239,131 @@ def rank_program(g, core, T, topo):
         x = mm(T.pr[:, 0:P], P, "qr", 128 * t, "H%d" % (t - 1), 0, (trc[t], trs[t], tsq))
         return func(T.sqn[:], T.pr[:, 0:P], F.Square, x, *deps)
 
+    def score(t, h):
+        tc[h] = mm(T.pc[:, 512 * h:512 * h + 128], 128, "H%d" % t, 128 * h, "qk", 0, (hc[h], hs[h], tq, tv[h]))
+
+    def use(t, h):
+        s = T.pc[:, 512 * h + t:512 * h + t + 1]
+        if t:
+            tv[h] = ts(uses[h], s, s, T.us[:, h:h + 1], A.mult, A.add, tc[h], tus)
+        else:
+            tv[h] = ts(uses[h], s, s, None, A.mult, None, tc[h])
+
+    def add_up(h, tx):
+        x = 384 * h
+        return scan(T.SO[:, x:x + 384], T.G[:], T.X[:, x:x + 384], A.mult, A.add, tx, tk, tcon)
+
+    def keep(h, to):
+        return ts(T.us[:, h:h + 1], order[h], float(K), uses[h], A.is_ge, A.mult, to)
+
+    def mark(h, to):
+        return ts(T.E[:, 128 * h:128 * h + 128], T.Z[:], order[h], T.pl[:, h:h + 1], A.is_equal, A.mult, to, tz)
+
+    def stays(h, to):
+        return ts(T.st[:, h:h + 1], order[h], float(K), float(P), A.is_ge, A.mult, to)
+
+    def slot(h, x):
+        return ts(T.sl[:, h:h + 1], order[h], T.st[:, h:h + 1], T.plk[:, h:h + 1], A.add, A.min, x)
+
+    def lay(h, x):
+        return ts(T.Y[:, 128 * h:128 * h + 128], T.JG[:], T.sl[:, h:h + 1], -float(K), A.add, A.max, x)
+
+    for h in range(2):
+        score(0, h)
+    for h in range(2):
+        use(0, h)
+
     for t in range(R):
         H, M, S = "H%d" % t, "M%d" % t, "S%d" % t
         last = t == R - 1
         u = t * P
-        tc = [mm(T.pc[:, 512 * h:512 * h + 128], 128, H, 128 * h, "qk", 0, (hc[h], hs[h], tq, tv[h])) for h in range(2)]
-        a = P - K if last else 0
+        n = K if last else P
         wait("y", hc[1], hs[1])
-        syn.dma_start(u8(T[M][:, a:P]), u8(T[H][:, a:P])).then_inc(T.sem["cp%d" % t], 16)
-        syn.dma_start(T[M + "s"][:, a:P], T[H + "s"][:, a:P]).then_inc(T.sem["cp%d" % t], 16)
-        if t > 1 and not last:
+        syn.dma_start(u8(T[M][:, K:K + n]), u8(T[H][:, 0:n])).then_inc(T.sem["cp%d" % t], 16)
+        syn.dma_start(T[M + "s"][:, K:K + n], T[H + "s"][:, 0:n]).then_inc(T.sem["cp%d" % t], 16)
+        if not last:
             tsq = ahead(t + 1, tadd)
         if t == 1:
             for o in range(O):
                 z = mm(T.py[:, 512 * o:512 * o + P], P, "wk", 128 * o, "H0", 0, (tw,))
-                tyw[o] = tyc[o] = func(T.yw[:, o * W:o * W + P], T.py[:, 512 * o:512 * o + P], F.Copy, z)
+                tyw[o] = tyc[o] = func(T.yw[:, o * W + K:o * W + W], T.py[:, 512 * o:512 * o + P], F.Copy, z)
         if t:
             products(t - 1, tm)
-        tb = []
-        uses = [T.uc[:, h:h + 1] for h in range(2)]
-
-        def use(h):
-            s = T.pc[:, 512 * h + t:512 * h + t + 1]
-            if t:
-                tv[h] = ts(uses[h], s, s, T.us[:, h:h + 1], A.mult, A.add, tc[h], tus_old)
-            else:
-                tv[h] = ts(uses[h], s, s, None, A.mult, None, tc[h])
-
-        def equal(h):
-            return ts(T.X[:, 416 * h:416 * h + 128], T.U[:, u + 128 * h:u + 128 * h + 128], uses[h], None, A.is_equal, None, tv[h], tu)
-
-        def add_up(h, tx):
-            x = 416 * h
-            return scan(T.SO[:, x:x + 385], T.G[:, x:x + 385], T.X[:, x:x + 385], A.mult, A.add, tx, tk, tcon)
-
-        def spread(h, to):
-            tr = turn(T.RT[:, 32 * h:32 * h + 32], T.SO[:, 416 * h + 384:416 * h + 416], to)
-            wait("g", tr)
-            for a in range(4):
-                tb.append(done("g", g.partition_broadcast(T.RB[:, 128 * h + 32 * a:128 * h + 32 * a + 32], T.RT[32 * a:32 * a + 1, 32 * h:32 * h + 32], 128)))
-
-        def keep(h, to):
-            return ts(T.us[:, h:h + 1], T.SO[:, 416 * h + 384:416 * h + 385], float(K), uses[h], A.is_ge, A.mult, to)
-
-        def mark(h, to):
-            return ts(T.E[:, 128 * h:128 * h + 128], T.Z[:], T.SO[:, 416 * h + 384:416 * h + 385], T.pl[:, h:h + 1], A.is_equal, A.mult, to, tz)
-
-        def twice(h):
-            return func(T.du[:, 256 * h:256 * h + 256], T.RB[:, 128 * h:128 * h + 128].indirect(T.dl[:]), F.Copy, tb[4 * h + 3], tdl)
-
-        tus_old = tus
-        use(0)
-        equal(0)
+        ts(T.X[:, 0:128], T.U[:, u:u + 128], uses[0], None, A.is_equal, None, tv[0], tu)
         ts(T.X[:, 128:256], T.U[:, u:u + 128], uses[0], None, A.is_le, None)
-        tx = ts(T.X[:, 256:384], T.U[:, u + 128:u + 256], uses[0], None, A.is_lt, None)
-        use(1)
-        to0 = add_up(0, tx)
-        equal(1)
-        spread(0, to0)
-        tx = ts(T.X[:, 416 + 128:416 + 384], T.U[:, u:u + 256], uses[1], None, A.is_le, None)
-        x0 = mark(0, to0)
-        to = add_up(1, tx)
-        turn(T.ET[:, 0:P:2], T.E[:, 0:128], x0)
-        if t == 0:
-            tsq = ahead(1)
-            trs[2] = picks("qr", "qk", 256, 384, 0, 128, T.offq[:, 16:24], (toff[2],))
-        td = [twice(0)]
-        x = mark(1, to)
-        spread(1, to)
-        x = turn(T.ET[:, 1:P:2], T.E[:, 128:256], x)
-        if not last:
-            keep(0, to0)
-        x = scan(T.ES[:], T.ER[:], T.ET[:], A.mult, A.add, x, ter)
-        if not last:
-            tus = keep(1, to)
-        x = tt(T.fa[0:64, :], T.ES[0:64, K - 1:P:K], T.ES[64:128, K - 1:P:K], A.add, x)
-        x = tt(T.fb[0:32, :], T.fa[0:32, :], T.fa[32:64, :], A.add, x)
+        x0 = ts(T.X[:, 256:384], T.U[:, u + 128:u + 256], uses[0], None, A.is_lt, None)
+        ts(T.X[:, 384:512], T.U[:, u + 128:u + 256], uses[1], None, A.is_equal, None, tv[1])
+        x1 = ts(T.X[:, 512:768], T.U[:, u:u + 256], uses[1], None, A.is_le, None)
+        to = [add_up(0, x0), add_up(1, x1)]
+        e0 = mark(0, to[0])
+        s0 = stays(0, to[0])
+        e1 = mark(1, to[1])
+        s1 = stays(1, to[1])
+        turn(T.ET[:, 0:P:2], T.E[:, 0:128], e0)
+        s0 = slot(0, s0)
+        x = turn(T.ET[:, 1:P:2], T.E[:, 128:256], e1)
+        s1 = slot(1, s1)
+        s0 = lay(0, s0)
+        x = scan(T.ES[:], T.ER[:], T.ET[:], A.mult, A.add, x)
+        s1 = lay(1, s1)
+        turn(T.YT[:, 0:128], T.Y[:, 0:128], s0)
+        x = fold(T.fa, T.fb, (T.ES[0:64, K - 1:P:K], T.ES[64:128, K - 1:P:K]), A.add, x)
         for a in range(4):
             tl = copy(T.lst[32 * a:32 * a + 32, 4 * t:4 * t + 4], T.fb[0:32, :], x)
         lst = T.lst[:, 4 * t:4 * t + 4]
+        s1 = turn(T.YT[:, 128:256], T.Y[:, 128:256], s1)
         if t == 0:
             wait("g", tl)
             send(T.lland[:], lst, "arl", t)
         else:
             x = pick(S, H, 0, K, 0, P, lst, (tl,))
             z = picks(S, H, 0, K, 0, P, lst, (tl,))
-            wait("g", x)
-            send(u8(T[M][:, P:W]), u8(T[S][:]), "arc%d" % t, t)
             wait("g", z)
-            send(T[M + "s"][:, P:W], T[S + "s"][:], "ars%d" % t, t)
-        td.append(twice(1))
-        if t == 1:
-            trc[2] = pick("qr", "qk", 256, 384, 0, 128, T.offq[:, 16:24], (toff[2],))
-            tsq = ahead(2, tadd)
-        x = turn(T.du2[:], T.du[:], *td)
-        ts(T.ma[:], T.du2[:, 0:512:32], float(P), None, A.add, None, x)
-        x = ts(T.mb[:], T.du2[:, 0:512:32], float(K), None, A.is_lt, None)
-        x = tt(T.mc[:], T.ma[:], T.mb[:], A.mult, x)
-        x = tt(T.md[:], T.mc[:], T.fc[:], A.max, x)
-        mrg = T.mrg[:, 16 * t:16 * t + 16]
-        tm = copy(mrg, T.md[:], x)
-        if not last:
-            tadd = tt(T.U[:, u + P:u + 2 * P], T.U[:, u:u + P], T.sqn[:], A.add, tsq, tu)
-        if t and t + 2 < R:
-            query(t + 2, fill(T.offq[:, 8 * t + 16:8 * t + 24], t + 2))
+            send(T[M + "s"][:, 0:K], T[S + "s"][:], "ars%d" % t, t)
+            wait("g", x)
+            send(u8(T[M][:, 0:K]), u8(T[S][:]), "arc%d" % t, t)
+        if t + 2 < R:
+            query_scales(t + 2)
+        todo = [] if last else [0, 1]
+
+        def carry():
+            if todo:
+                a = 128 * todo.pop(0)
+                return tt(T.U[:, u + P + a:u + P + a + 128], T.U[:, u + a:u + a + 128], T.sqn[:, a:a + 128], A.add, tsq, tu)
+            return tadd
+
+        if t == 0:
+            carry()
+        x = scan(T.YS[:], T.YR[:], T.YT[:], A.add, A.max, s1)
+        tadd = carry()
+        x = fold(T.ya, T.yb, (T.YS[0:64, 15:P:16], T.YS[64:128, 15:P:16]), A.max, x)
         if t == 0:
             z = came("arl", t)
-            arr[t] = (pick(M, "far", P, W, 0, P, T.lland[:], (z, arr[t][0])), picks(M, "far", P, W, 0, P, T.lland[:], (z, arr[t][1])))
+            wait("v", x)
+            arr[t] = (pick(M, "far", 0, K, 0, P, T.lland[:], (z, arr[t][0])), picks(M, "far", 0, K, 0, P, T.lland[:], (z, arr[t][1])))
+        for a in range(4):
+            tm = ts(T.mrg[32 * a:32 * a + 32, 16 * t:16 * t + 16], T.yb[0:32, :], float(K), None, A.add, None, x)
+        if not last:
+            keep(0, to[0])
+            tus = keep(1, to[1])
+        tadd = carry()
         if not last:
             ac, as_ = arr[t]
             cp = ("cp%d" % t, 32)
             n = "H%d" % (t + 1)
-            z = mm(T.pa[:, 0:128], 128, "qr", 128 * (t + 1), M, W - 128, (ac, as_, cp, trc[t + 1], trs[t + 1], tsqa))
+            z = mm(T.pa[:, 0:128], 128, "qr", 128 * (t + 1), M, 0, (ac, as_, cp, trc[t + 1], trs[t + 1], tsqa))
             hc, hs = [], []
             for h in range(2):
                 off = T.mrg[:, 16 * t + 8 * h:16 * t + 8 * h + 8]
                 hc.append(pick(n, M, 128 * h, 128 * h + 128, 0, W, off, (ac, cp, tm)))
                 hs.append(picks(n, M, 128 * h, 128 * h + 128, 0, W, off, (as_, cp, tm)))
-                if h == 0:
-                    tsqa = func(T.sqa[:], T.pa[:, 128 - K:128], F.Square, z, tu)
+                score(t + 1, h)
+            tsqa = func(T.sqa[:], T.pa[:, 0:K], F.Square, z, tu)
+            if t + 2 < R:
+                query_codes(t + 2)
+            use(t + 1, 0)
             tu = copy(T.U[:, u + P:u + 2 * P].indirect(lst), T.sqa[:], tadd, tsqa)
+            use(t + 1, 1)
         else:
             products(t, tm)
 

@@ -3,7 +3,9 @@ from concourse.mybir import dt, AluOpType, ActivationFunctionType
 P, K, R, O = 256, 64, 6, 2
 PART = [1, 2, 1, 2, 1, 2]
 W = K + P
-FAR = 1024.0
+QW = 32
+STAY = 1024.0
+FAR = 4096.0
 CODE, PLANE = "float8_e4m3fn_x4", "uint8"
 
 SCRATCH = {
@@ -13,38 +15,41 @@ SCRATCH = {
     "qk": ("sbuf", [128, 128], CODE), "qks": ("sbuf", [128, 128], PLANE),
     "qr": ("sbuf", [128, 128 * R], CODE), "qrs": ("sbuf", [128, 128 * R], PLANE),
     "wk": ("sbuf", [128, 128 * O], CODE), "wks": ("sbuf", [128, 128 * O], PLANE),
-    "far": ("sbuf", [128, P], CODE), "fars": ("sbuf", [128, P], PLANE),
+    "N2": ("sbuf", [128, P + 2 * K], CODE), "N2s": ("sbuf", [128, P + 2 * K], PLANE),
     "offq": ("sbuf", [128, 8 * R], "uint16"),
     "lst": ("sbuf", [128, R * K // 16], "uint16"),
-    "lland": ("sbuf", [128, K // 16], "uint16"),
     "mrg": ("sbuf", [128, R * P // 16], "uint16"),
+    "own": ("sbuf", [128, 4], "uint16"),
     "U": ("sbuf", [128, R * P], "float32"),
+    "US": ("sbuf", [128, W], "float32"),
+    "UD": ("sbuf", [128, K], "float32"),
+    "UT": ("sbuf", [128, K], "float32"),
     "sqn": ("sbuf", [128, P], "float32"),
-    "sqa": ("sbuf", [128, K], "float32"),
+    "sqf": ("sbuf", [128, 2 * P], "float32"),
     "uc": ("sbuf", [128, 2], "float32"),
     "us": ("sbuf", [128, 2], "float32"),
-    "X": ("sbuf", [128, 768], "bfloat16"),
-    "G": ("sbuf", [128, 384], "bfloat16"),
-    "SO": ("sbuf", [128, 768], "bfloat16"),
-    "Z": ("sbuf", [128, 128], "bfloat16"),
+    "X": ("sbuf", [128, 640], "bfloat16"),
+    "G": ("sbuf", [128, 640], "bfloat16"),
+    "SO": ("sbuf", [128, 640], "bfloat16"),
+    "sgn": ("sbuf", [128, P], "bfloat16"),
+    "sa": ("sbuf", [128, 1], "float32"),
+    "Z": ("sbuf", [128, P], "bfloat16"),
     "E": ("sbuf", [128, P], "bfloat16"),
-    "ET": ("sbuf", [128, P], "bfloat16"),
-    "ER": ("sbuf", [128, P], "bfloat16"),
-    "ES": ("sbuf", [128, P], "bfloat16"),
-    "fa": ("sbuf", [128, 4], "bfloat16"),
+    "ET": ("sbuf", [128, 2 * P], "bfloat16"),
+    "ER": ("sbuf", [128, 2 * P], "bfloat16"),
+    "ES": ("sbuf", [128, 2 * P], "bfloat16"),
     "fb": ("sbuf", [128, 4], "bfloat16"),
-    "pl": ("sbuf", [128, 2], "bfloat16"),
+    "num": ("sbuf", [128, 2 * (R - 1)], "bfloat16"),
     "plk": ("sbuf", [128, 2], "float32"),
     "st": ("sbuf", [128, 2], "float32"),
-    "sl": ("sbuf", [128, 2], "float32"),
-    "J": ("sbuf", [128, 128], "bfloat16"),
-    "JG": ("sbuf", [128, 128], "bfloat16"),
-    "Y": ("sbuf", [128, P], "bfloat16"),
-    "YT": ("sbuf", [128, P], "bfloat16"),
-    "YR": ("sbuf", [128, P], "bfloat16"),
-    "YS": ("sbuf", [128, P], "bfloat16"),
-    "ya": ("sbuf", [128, 16], "bfloat16"),
-    "yb": ("sbuf", [128, 16], "bfloat16"),
+    "sl": ("sbuf", [128, 2 * R], "float32"),
+    "J": ("sbuf", [128, 32], "bfloat16"),
+    "JG": ("sbuf", [128, 32], "bfloat16"),
+    "Y": ("sbuf", [128, 64], "bfloat16"),
+    "YT": ("sbuf", [128, 64], "bfloat16"),
+    "YR": ("sbuf", [128, 64], "bfloat16"),
+    "YS": ("sbuf", [128, 64], "bfloat16"),
+    "yb": ("sbuf", [128, 2, 8], "bfloat16"),
     "iq": ("sbuf", [128, 8 * R], "int32"),
     "ip": ("sbuf", [128, 1], "int32"),
     "ipm": ("sbuf", [128, 1], "int32"),
@@ -52,15 +57,19 @@ SCRATCH = {
     "yw": ("sbuf", [128, (R + 1) * O * W], "float32"),
     "pc": ("psum", [128, 1024], "float32"),
     "pa": ("psum", [128, 512], "float32"),
-    "pr": ("psum", [128, 512], "float32"),
+    "pr": ("psum", [128, 1024], "float32"),
     "py": ("psum", [128, 512 * O], "float32"),
 }
-SEMAPHORES = ["sv", "ss", "sp", "sg", "ldc", "ldq", "ldw", "loc", "sty", "arl"]
+SEMAPHORES = ["sv", "ss", "sp", "sg", "ld0", "ld1", "ldq", "ldw", "loc", "sty", "end", "cpn"]
 for _t in range(R):
-    for _n, _w in (("H", P), ("M", W), ("S", K)):
+    _stages = [("H", P), ("M", W), ("S", K) if _t % 2 else ("F", P + K * _t)]
+    for _n, _w in _stages:
         SCRATCH["%s%d" % (_n, _t)] = ("sbuf", [128, _w], CODE)
         SCRATCH["%s%ds" % (_n, _t)] = ("sbuf", [128, _w], PLANE)
     SEMAPHORES += [_n + str(_t) for _n in ("cp", "arc", "ars")]
+    if _t % 2 == 0:
+        SCRATCH["L%d" % _t] = ("sbuf", [128, K // 16], "uint16")
+        SEMAPHORES += [_n + str(_t) for _n in ("arl", "cpf")]
 
 
 def rank_program(g, core, T, topo):
@@ -90,27 +99,40 @@ def rank_program(g, core, T, topo):
         ins.then_inc(T.sem[own[q]], 1)
         return (own[q], count[q])
 
-    def send(out_ap, in_ap, sem, t):
-        dst = T.cores[rank ^ PART[t]]
-        rid, pid = topo.addr(dst)[:2]
-        g.remote_dma(out_ap=out_ap, in_ap=in_ap, remote_sem=T.sem[sem], local_sem=T.sem["loc"], pid=pid, routing_id=rid, dma_engine_mask=topo.mask(core, dst))
-        sent[0] += len(topo.engines(core, dst))
-
-    def came(sem, t):
-        return (sem, len(topo.engines(T.cores[rank ^ PART[t]], core)))
-
     def u8(v):
         return v.bitcast(dt.uint8)
 
-    def pick(out, win, a, b, c, d, off, deps):
+    def send(out_ap, in_ap, sem, t, *deps):
+        wait("g", *deps)
+        dst = T.cores[rank ^ PART[t]]
+        rid, pid = topo.addr(dst)[:2]
+        g.remote_dma(out_ap=out_ap, in_ap=in_ap, remote_sem=T.sem[sem + str(t)], local_sem=T.sem["loc"], pid=pid, routing_id=rid, dma_engine_mask=topo.mask(core, dst))
+        sent[0] += len(topo.engines(core, dst))
+
+    def send_columns(out, src, n, t, codes, scales):
+        send(T[out + "s"][:, 0:n], T[src + "s"][:, 0:n], "ars", t, *scales)
+        send(u8(T[out][:, 0:n]), u8(T[src][:, 0:n]), "arc", t, *codes)
+
+    def came(sem, t):
+        return (sem + str(t), len(topo.engines(T.cores[rank ^ PART[t]], core)))
+
+    def lay_beside(out, a, src, b, n, sem, *deps):
+        wait("y", *deps)
+        syn.dma_start(u8(T[out][:, a:a + n]), u8(T[src][:, b:b + n])).then_inc(T.sem[sem], 16)
+        syn.dma_start(T[out + "s"][:, a:a + n], T[src + "s"][:, b:b + n]).then_inc(T.sem[sem], 16)
+
+    def held(t):
+        return ("cp%d" % t, 64 if t % 2 and t < R - 1 else 32)
+
+    def pick(out, a, n, win, off, *deps):
         wait("v", *deps)
-        return done("v", vec.tensor_copy(T[out][:, a:b].bitcast(dt.uint32), T[win][:, c:d].bitcast(dt.uint32).indirect(off)))
+        return done("v", vec.tensor_copy(T[out][:, a:a + n].bitcast(dt.uint32), T[win][:].bitcast(dt.uint32).indirect(off)))
 
-    def picks(out, win, a, b, c, d, off, deps):
+    def picks(out, a, n, win, off, *deps):
         wait("s", *deps)
-        return done("s", act.activation(T[out + "s"][:, a:b], T[win + "s"][:, c:d].indirect(off), F.Copy))
+        return done("s", act.activation(T[out + "s"][:, a:a + n], T[win + "s"][:].indirect(off), F.Copy))
 
-    def mm(out, n, st, a, mv, b, deps):
+    def mm(out, n, st, a, mv, b, *deps):
         wait("p", *deps)
         return done("p", ten.matmul_mx(out, T[st][:, a:a + 128], T[st + "s"][:, a:a + 128], T[mv][:, b:b + n], T[mv + "s"][:, b:b + n], True, True))
 
@@ -128,9 +150,9 @@ def rank_program(g, core, T, topo):
         wait("v", *deps)
         return done("v", vec.tensor_tensor(out, in0, in1, op))
 
-    def scan(out, d0, d1, op0, op1, *deps):
+    def scan(out, d0, d1, first, op0, op1, *deps):
         wait("v", *deps)
-        return done("v", vec.tensor_tensor_scan(out, d0, d1, 0.0, op0, op1))
+        return done("v", vec.tensor_tensor_scan(out, d0, d1, first, op0, op1))
 
     def turn(out, in_, *deps):
         wait("v", *deps)
@@ -140,6 +162,10 @@ def rank_program(g, core, T, topo):
         wait("v", *deps)
         return done("v", vec.tensor_copy(out, in_))
 
+    def quantize(out, a, n, src, *deps):
+        wait("v", *deps)
+        return done("v", vec.quantize_mx(T[out][:, a:a + n], T[out + "s"][:, a:a + n], src[:, 4 * a:4 * a + 4 * n]))
+
     def func(out, in_, f, *deps):
         wait("s", *deps)
         return done("s", act.activation(out, in_, f))
@@ -147,181 +173,205 @@ def rank_program(g, core, T, topo):
     def iota(out, pattern, base, step):
         return done("g", g.iota(out, pattern, base, step, allow_small_or_imprecise_dtypes=True))
 
-    def fold(half, quarter, src, op, dep):
-        x = tt(half[0:64, :], src[0], src[1], op, dep)
-        return tt(quarter[0:32, :], half[0:32, :], half[32:64, :], op, x)
-
-    act.dma_start(T.qin[:], T.qt[:]).then_inc(T.sem.ldq, 16)
-    syn.dma_start(T.cin[:], T.c[:]).then_inc(T.sem.ldc, 16)
+    act.dma_start(T.qin[:, 0:QW], T.qt[:, 0:QW]).then_inc(T.sem.ldq, 16)
+    for h in range(2):
+        syn.dma_start(T.cin[:, 512 * h:512 * h + 512], T.c[:, 512 * h:512 * h + 512]).then_inc(T.sem["ld%d" % h], 16)
     syn.dma_start(T.win[:], T.w[:]).then_inc(T.sem.ldw, 16)
+    tq = fill(T.qin[:, QW:512], 0.0)
     tg1 = fill(T.G[:], 1.0)
     tiq = done("g", g.iota(T.iq[:], [[1, R], [0, 8]], 0, 0))
     tip = done("g", g.iota(T.ip[:], [[1, 1]], 0, 1))
+    tj = iota(T.J[:], [[0, 2], [1, 16]], 0, 0)
     wait("g", tg1)
-    tk = done("g", g.affine_select(T.G[:, 0:128], T.G[:, 0:128], [[-1, 128]], A.not_equal, 0.0, 0, 1))
-    tj = iota(T.J[:], [[32, 4], [0, 2], [1, 16]], 0, 0)
-    iota(T.Z[:], [[16, 4], [0, 2], [1, 16]], 0, 0)
-    iota(T.pl[:], [[128, 2]], 0, 1)
-    tz = iota(T.plk[:], [[128, 2]], K, 1)
-    fill(T.ER[:], 1.0)
-    ter = fill(T.YR[:], 0.0)
+    done("g", g.affine_select(T.G[:, 0:128], T.G[:, 0:128], [[-1, 128]], A.not_equal, 0.0, 0, 1))
+    tk = done("g", g.affine_select(T.G[:, 512:640], T.G[:, 512:640], [[-1, 128]], A.not_equal, -1.0, 0, 1))
+    iota(T.Z[:, 0:128], [[16, 4], [0, 2], [1, 16]], 0, 0)
+    iota(T.Z[:, 128:256], [[-32, 4], [0, 2], [-2, 16]], P, 0)
+    iota(T.num[:, 0:2], [[128, 2]], 0, 1)
+    tz = iota(T.plk[:], [[128, 2]], 0, 1)
     toff = copy(T.offq[:], T.iq[:], tiq)
-    ta = ts(T.ipm[:], T.ip[:], 16, None, A.bitwise_and, None, tip)
+    ta = ts(T.ipm[:], T.ip[:], 15, None, A.bitwise_and, None, tip)
+    fill(T.YR[:], 0.0)
+    ter = fill(T.ER[:], 1.0)
+    ta = copy(T.idf[:], T.ipm[:], ta)
     fill(T.G[:, 128:129], -1.0, ter)
-    fill(T.ER[:, 0:P:K], 0.0)
-    fill(T.YR[:, 0:P:16], -FAR)
-    ta = tt(T.idf[:], T.ip[:], T.ipm[:], A.subtract, ta)
+    fill(T.ER[:, 0:2 * P:2 * K], 0.0)
+    fill(T.YR[:, 0:64:16], -FAR)
 
-    wait("v", ("ldq", 16))
-    tq = done("v", vec.quantize_mx(T.qk[:], T.qks[:], T.qin[:]))
-    ta = ts(T.JG[:], T.J[:], T.idf[:], FAR - K, A.is_equal, A.mult, ta, tj)
     trc, trs = [None] * R, [None] * R
 
     def query_codes(t):
-        trc[t] = pick("qr", "qk", 128 * t, 128 * t + 128, 0, 128, T.offq[:, 8 * t:8 * t + 8], (tq, toff))
+        trc[t] = pick("qr", 128 * t, 128, "qk", T.offq[:, 8 * t:8 * t + 8], tq, toff)
 
     def query_scales(t):
-        trs[t] = picks("qr", "qk", 128 * t, 128 * t + 128, 0, 128, T.offq[:, 8 * t:8 * t + 8], (tq, toff))
+        trs[t] = picks("qr", 128 * t, 128, "qk", T.offq[:, 8 * t:8 * t + 8], tq, toff)
 
+    tq = quantize("qk", 0, 128, T.qin, ("ldq", 16), tq)
+    ta = ts(T.JG[:], T.J[:], T.idf[:], FAR + K, A.is_equal, A.mult, ta, tj)
     query_codes(0)
     query_scales(0)
     query_scales(1)
-    wait("v", ("ldc", 16))
-    x = done("v", vec.quantize_mx(T.H0[:], T.H0s[:], T.cin[:]))
-    hc = hs = [x, x]
+    hc = [quantize("H0", 128 * h, 128, T.cin, ("ld%d" % h, 16)) for h in range(2)]
+    hs = list(hc)
+    send_columns("F0", "H0", P, 0, hc, hc)
+    tu = []
+    for h in range(2):
+        x = mm(T.pr[:, 512 * h:512 * h + 128], 128, "qr", 0, "H0", 128 * h, trc[0], trs[0], hc[h])
+        tu.append(func(T.U[:, 128 * h:128 * h + 128], T.pr[:, 512 * h:512 * h + 128], F.Square, x))
 
-    wait("g", x)
-    send(u8(T.far[:]), u8(T.H0[:]), "arc0", 0)
-    send(T.fars[:], T.H0s[:], "ars0", 0)
-
-    t0 = mm(T.pr[:, 0:P], P, "qr", 0, "H0", 0, (trc[0], trs[0], x))
-    tu = func(T.U[:, 0:P], T.pr[:, 0:P], F.Square, t0)
-    tcon = ts(T.JG[:], T.JG[:], -FAR, None, A.add, None, ta)
-    query_codes(1)
-    wait("v", ("ldw", 16))
-    tw = done("v", vec.quantize_mx(T.wk[:], T.wks[:], T.win[:]))
-
-    tsqa = tm = tadd = tus = None
+    tm = tadd = tus = tsqa = tsqf = None
     tv = [None, None]
     tc = [None, None]
     tyc = [None, None]
     tyw = [None, None]
-    tsq = tu
-    arr = [(came("arc%d" % t, t), came("ars%d" % t, t)) for t in range(R)]
-    uses = [T.uc[:, h:h + 1] for h in range(2)]
-    order = [T.SO[:, 384 * h + 383:384 * h + 384] for h in range(2)]
+    tsq = tu[0]
+    tnum = [None] * R
+    arr = [(came("arc", t), came("ars", t)) for t in range(R)]
+    far = {0: arr[0]}
+    order = [T.SO[:, 383:384], T.SO[:, 639:640]]
+    stores = []
 
     def products(t, tm):
-        z = [mm(T.py[:, 512 * o:512 * o + 128], 128, "wk", 128 * o, "M%d" % t, 0, (tw, arr[t][0], arr[t][1], ("cp%d" % t, 32), tyc[o])) for o in range(O)]
         tail = t == R - 1
-        for o in range(O):
+        z = {}
+        for o in range(O - 1, -1, -1):
+            z[o] = mm(T.py[:, 512 * o:512 * o + 128], 128, "wk", 128 * o, "M%d" % t, 0, tw, arr[t][0], arr[t][1], held(t), tyc[o])
+        for o in z:
             b = (t * O + o) * W
             src = T.py[:, 512 * o:512 * o + K]
-            z[o] = copy(T.yw[:, b:b + K], src, z[o]) if tail else z[o]
-        for o in range(O):
+            tyc[o] = copy(T.yw[:, b:b + K], src, z[o]) if tail else func(T.yw[:, b:b + K], src, F.Copy, z[o])
+        for o in z:
             b = (t * O + o) * W
-            n = ((t + 1) * O + o) * W + K
-            src = T.py[:, 512 * o:512 * o + K]
-            win = T.yw[:, b:b + W].indirect(T.mrg[:, 16 * t:16 * t + 16])
-            x = z[o]
-            if not tail:
-                tyc[o] = x = func(T.yw[:, b:b + K], src, F.Copy, x)
+            n = b + O * W + K
             if tail and o == 0:
-                x = copy(T.yw[:, n:n + P], win, x, tyw[o], tm)
+                n = b + K
+                x = copy(T.yw[:, n:n + P].indirect(T.lst[:, 4 * t:4 * t + 4]), T.yw[:, b:b + K], tyc[o], ("sty", 16 * t * O))
             else:
-                x = func(T.yw[:, n:n + P], win, F.Copy, x, tyw[o], tm)
+                x = func(T.yw[:, n:n + P], T.yw[:, b:b + W].indirect(T.mrg[:, 16 * t:16 * t + 16]), F.Copy, tyc[o], tyw[o], tm)
             tyw[o] = x
-            q = "s" if tail and o == 1 else "y"
-            wait(q, x)
-            queue[q].dma_start(T.y[:, (t * O + o) * P:(t * O + o) * P + P], T.yw[:, n:n + P]).then_inc(T.sem.sty, 16)
+            stores.append(("s" if tail and o == 1 else "y", (t * O + o) * P, n, x, "end" if tail else "sty"))
+
+    def store(*deps):
+        while stores:
+            q, a, n, x, sem = stores.pop(0)
+            wait(q, x, *deps)
+            queue[q].dma_start(T.y[:, a:a + P], T.yw[:, n:n + P]).then_inc(T.sem[sem], 16)
 
     def ahead(t, *deps):
-        x = mm(T.pr[:, 0:P], P, "qr", 128 * t, "H%d" % (t - 1), 0, (trc[t], trs[t], tsq))
+        x = mm(T.pr[:, 0:P], P, "qr", 128 * t, "H%d" % (t - 1), 0, trc[t], trs[t], tsq, hc[1], hs[1])
         return func(T.sqn[:], T.pr[:, 0:P], F.Square, x, *deps)
 
     def score(t, h):
-        tc[h] = mm(T.pc[:, 512 * h:512 * h + 128], 128, "H%d" % t, 128 * h, "qk", 0, (hc[h], hs[h], tq, tv[h]))
+        tc[h] = mm(T.pc[:, 512 * h:512 * h + 128], 128, "H%d" % t, 128 * h, "qk", 0, hc[h], hs[h], tq, tv[h])
 
     def use(t, h):
         s = T.pc[:, 512 * h + t:512 * h + t + 1]
         if t:
-            tv[h] = ts(uses[h], s, s, T.us[:, h:h + 1], A.mult, A.add, tc[h], tus)
+            tv[h] = ts(T.uc[:, h:h + 1], s, s, T.us[:, h:h + 1], A.mult, A.add, tc[h], tus)
         else:
-            tv[h] = ts(uses[h], s, s, None, A.mult, None, tc[h])
+            tv[h] = ts(T.uc[:, h:h + 1], s, s, None, A.mult, None, tc[h])
 
-    def add_up(h, tx):
-        x = 384 * h
-        return scan(T.SO[:, x:x + 384], T.G[:], T.X[:, x:x + 384], A.mult, A.add, tx, tk, tcon)
+    def staying(out, h, x, to):
+        return ts(out[:, h:h + 1], order[h], float((K, P - 2 * K)[h]), x, (A.is_ge, A.is_le)[h], A.mult, to)
 
-    def keep(h, to):
-        return ts(T.us[:, h:h + 1], order[h], float(K), uses[h], A.is_ge, A.mult, to)
+    def mark(t, h, to):
+        c = h if t % 2 else 2 * t + h
+        return ts(T.E[:, 128 * h:128 * h + 128], T.Z[:, 128 * h:128 * h + 128], order[h], T.num[:, c:c + 1], A.is_equal, A.mult, to, tz, tnum[t])
 
-    def mark(h, to):
-        return ts(T.E[:, 128 * h:128 * h + 128], T.Z[:], order[h], T.pl[:, h:h + 1], A.is_equal, A.mult, to, tz)
+    def slot(t, h, x):
+        if h:
+            return ts(T.sl[:, 2 * t + 1:2 * t + 2], order[1], -0.5, T.st[:, 1:2], A.mult, A.add, x)
+        return ts(T.sl[:, 2 * t:2 * t + 1], order[0], T.st[:, 0:1], -128.0, A.add, A.add, x)
 
-    def stays(h, to):
-        return ts(T.st[:, h:h + 1], order[h], float(K), float(P), A.is_ge, A.mult, to)
+    def lay(t, h, x):
+        return ts(T.Y[:, 32 * h:32 * h + 32], T.JG[:], T.sl[:, 2 * t + h:2 * t + h + 1], T.plk[:, h:h + 1], A.add, A.min, x)
 
-    def slot(h, x):
-        return ts(T.sl[:, h:h + 1], order[h], T.st[:, h:h + 1], T.plk[:, h:h + 1], A.add, A.min, x)
+    def number(t, *deps):
+        for h in range(2):
+            c = 2 * t + h
+            tnum[t + 1] = ts(T.num[:, c + 2:c + 3], T.sl[:, c:c + 1], float(128 - K * (t + 1)), T.num[:, c:c + 1], A.add, A.min, *deps)
+        return tnum[t + 1]
 
-    def lay(h, x):
-        return ts(T.Y[:, 128 * h:128 * h + 128], T.JG[:], T.sl[:, h:h + 1], -float(K), A.add, A.max, x)
+    def merge_codes(t, h):
+        hc[h] = pick("H%d" % (t + 1), 128 * h, 128, "M%d" % t, T.mrg[:, 16 * t + 8 * h:16 * t + 8 * h + 8], arr[t][0], held(t), tm)
+
+    def merge_scales(t, h):
+        hs[h] = picks("H%d" % (t + 1), 128 * h, 128, "M%d" % t, T.mrg[:, 16 * t + 8 * h:16 * t + 8 * h + 8], arr[t][1], held(t), tm)
 
     for h in range(2):
         score(0, h)
+    tcon = ts(T.JG[:], T.JG[:], -FAR, None, A.add, None, ta)
+    query_codes(1)
+    query_codes(2)
+    tw = quantize("wk", 0, 128 * O, T.win, ("ldw", 16))
     for h in range(2):
         use(0, h)
 
     for t in range(R):
-        H, M, S = "H%d" % t, "M%d" % t, "S%d" % t
-        last = t == R - 1
-        u = t * P
-        n = K if last else P
-        wait("y", hc[1], hs[1])
-        syn.dma_start(u8(T[M][:, K:K + n]), u8(T[H][:, 0:n])).then_inc(T.sem["cp%d" % t], 16)
-        syn.dma_start(T[M + "s"][:, K:K + n], T[H + "s"][:, 0:n]).then_inc(T.sem["cp%d" % t], 16)
-        if not last:
-            tsq = ahead(t + 1, tadd)
-        if t == 1:
-            for o in range(O):
-                z = mm(T.py[:, 512 * o:512 * o + P], P, "wk", 128 * o, "H0", 0, (tw,))
-                tyw[o] = tyc[o] = func(T.yw[:, o * W + K:o * W + W], T.py[:, 512 * o:512 * o + P], F.Copy, z)
+        H, M, u = "H%d" % t, "M%d" % t, t * P
+        last, listed = t == R - 1, t % 2 == 0
+        if listed:
+            lay_beside(M, K, H, 0, P, "cp%d" % t, hc[1], hs[1])
+        uses = [T.uc[:, h:h + 1] if listed else T.UT[:, 32 * h:32 * h + 1] for h in range(2)]
+        wait("s", tv[1], *tu)
+        z = done("s", act.activation(T.sgn[:], T.U[:, u:u + P], F.Sign, bias=uses[1], scale=-1.0, accum_out=T.sa[:]))
+        ts(T.X[:, 0:128], T.U[:, u:u + 128], uses[0], None, A.is_equal, None, tv[0], tu[0])
+        ts(T.X[:, 128:256], T.U[:, u:u + 128], uses[0], None, A.is_le, None)
+        x0 = ts(T.X[:, 256:384], T.U[:, u + 128:u + 256], uses[0], None, A.is_lt, None, tu[1])
+        x1 = ts(T.X[:, 384:640], T.U[:, u:u + 256], uses[1], None, A.is_equal, None, tv[1])
+        to = [scan(T.SO[:, 0:384], T.G[:, 0:384], T.X[:, 0:384], 0.0, A.mult, A.add, x0, tk, tcon),
+              scan(T.SO[:, 384:640], T.G[:, 384:640], T.X[:, 384:640], T.sa[:], A.mult, A.add, x1, z)]
+        if not listed:
+            merge_scales(t - 1, 0)
+            lay_beside(M, K, H, 0, K if last else 128, "cp%d" % t, hc[0], hs[0])
+            if not last:
+                merge_scales(t - 1, 1)
         if t:
             products(t - 1, tm)
-        ts(T.X[:, 0:128], T.U[:, u:u + 128], uses[0], None, A.is_equal, None, tv[0], tu)
-        ts(T.X[:, 128:256], T.U[:, u:u + 128], uses[0], None, A.is_le, None)
-        x0 = ts(T.X[:, 256:384], T.U[:, u + 128:u + 256], uses[0], None, A.is_lt, None)
-        ts(T.X[:, 384:512], T.U[:, u + 128:u + 256], uses[1], None, A.is_equal, None, tv[1])
-        x1 = ts(T.X[:, 512:768], T.U[:, u:u + 256], uses[1], None, A.is_le, None)
-        to = [add_up(0, x0), add_up(1, x1)]
-        e0 = mark(0, to[0])
-        s0 = stays(0, to[0])
-        e1 = mark(1, to[1])
-        s1 = stays(1, to[1])
-        turn(T.ET[:, 0:P:2], T.E[:, 0:128], e0)
-        s0 = slot(0, s0)
-        x = turn(T.ET[:, 1:P:2], T.E[:, 128:256], e1)
-        s1 = slot(1, s1)
-        s0 = lay(0, s0)
-        x = scan(T.ES[:], T.ER[:], T.ET[:], A.mult, A.add, x)
-        s1 = lay(1, s1)
-        turn(T.YT[:, 0:128], T.Y[:, 0:128], s0)
-        x = fold(T.fa, T.fb, (T.ES[0:64, K - 1:P:K], T.ES[64:128, K - 1:P:K]), A.add, x)
-        for a in range(4):
-            tl = copy(T.lst[32 * a:32 * a + 32, 4 * t:4 * t + 4], T.fb[0:32, :], x)
-        lst = T.lst[:, 4 * t:4 * t + 4]
-        s1 = turn(T.YT[:, 128:256], T.Y[:, 128:256], s1)
-        if t == 0:
-            wait("g", tl)
-            send(T.lland[:], lst, "arl", t)
+        if last:
+            store()
+            merge_scales(t - 1, 1)
+        e0 = mark(t, 0, to[0])
+        s0 = staying(T.st, 0, STAY, to[0])
+        e1 = mark(t, 1, to[1])
+        s1 = staying(T.st, 1, STAY, to[1])
+        for h, e in enumerate((e0, e1)):
+            for a in range(2):
+                x = turn(T.ET[0:64, 2 * h + a:2 * P:4], T.E[64 * a:64 * a + 64, 128 * h:128 * h + 128], e)
+        if listed:
+            s0 = slot(t, 0, s0)
+            s1 = slot(t, 1, s1)
         else:
-            x = pick(S, H, 0, K, 0, P, lst, (tl,))
-            z = picks(S, H, 0, K, 0, P, lst, (tl,))
-            wait("g", z)
-            send(T[M + "s"][:, 0:K], T[S + "s"][:], "ars%d" % t, t)
-            wait("g", x)
-            send(u8(T[M][:, 0:K]), u8(T[S][:]), "arc%d" % t, t)
+            merge_codes(t - 1, 1)
+            if not last:
+                lay_beside(M, K + 128, H, 128, 128, "cp%d" % t, hc[1], hs[1])
+        if not last:
+            tsq = ahead(t + 1, tadd)
+        if t == 0:
+            for o in range(O):
+                z = mm(T.py[:, 512 * o:512 * o + P], P, "wk", 128 * o, "H0", 0, tw)
+                tyw[o] = tyc[o] = func(T.yw[:, o * W + K:o * W + W], T.py[:, 512 * o:512 * o + P], F.Copy, z)
+        x = scan(T.ES[0:64, :], T.ER[0:64, :], T.ET[0:64, :], 0.0, A.mult, A.add, x)
+        if listed:
+            s0 = lay(t, 0, s0)
+            s1 = lay(t, 1, s1)
+        else:
+            s0 = slot(t, 0, s0)
+            s1 = slot(t, 1, s1)
+        x = tt(T.fb[0:32, :], T.ES[0:32, 127:2 * P:128], T.ES[32:64, 127:2 * P:128], A.add, x)
+        lst = T.lst[:, 4 * t:4 * t + 4]
+        for a in range(4):
+            tl = ts(T.lst[32 * a:32 * a + 32, 4 * t:4 * t + 4], T.fb[0:32, :], float(K * t if listed else 0), None, A.add, None, x)
+        if listed:
+            send(T["L%d" % t][:], lst, "arl", t, tl)
+            n = P + K * t
+            x = mm(T.pa[:, 0:n], n, "qr", 128 * (t + 1), "F%d" % t, 0, trc[t + 1], trs[t + 1], tsqa, *far[t])
+            tsqa = tsqf = func(T.sqf[:, 0:n], T.pa[:, 0:n], F.Square, x)
+        else:
+            s0 = lay(t, 0, s0)
+            s1 = lay(t, 1, s1)
+            S = "S%d" % t
+            send_columns(M, S, K, t, (pick(S, 0, K, H, lst, tl),), (picks(S, 0, K, H, lst, tl, hs[1]),))
         if t + 2 < R:
             query_scales(t + 2)
         todo = [] if last else [0, 1]
@@ -329,45 +379,68 @@ def rank_program(g, core, T, topo):
         def carry():
             if todo:
                 a = 128 * todo.pop(0)
-                return tt(T.U[:, u + P + a:u + P + a + 128], T.U[:, u + a:u + a + 128], T.sqn[:, a:a + 128], A.add, tsq, tu)
+                out = T.US[:, K + a:K + a + 128] if listed else T.U[:, u + P + a:u + P + a + 128]
+                return tt(out, T.U[:, u + a:u + a + 128], T.sqn[:, a:a + 128], A.add, tsq, *tu)
             return tadd
 
-        if t == 0:
-            carry()
-        x = scan(T.YS[:], T.YR[:], T.YT[:], A.add, A.max, s1)
+        x = turn(T.YT[:], T.Y[:], s1)
+        carry()
+        x = scan(T.YS[:], T.YR[:], T.YT[:], 0.0, A.add, A.max, x)
         tadd = carry()
-        x = fold(T.ya, T.yb, (T.YS[0:64, 15:P:16], T.YS[64:128, 15:P:16]), A.max, x)
-        if t == 0:
-            z = came("arl", t)
-            wait("v", x)
-            arr[t] = (pick(M, "far", 0, K, 0, P, T.lland[:], (z, arr[t][0])), picks(M, "far", 0, K, 0, P, T.lland[:], (z, arr[t][1])))
         for a in range(4):
-            tm = ts(T.mrg[32 * a:32 * a + 32, 16 * t:16 * t + 16], T.yb[0:32, :], float(K), None, A.add, None, x)
-        if not last:
-            keep(0, to[0])
-            tus = keep(1, to[1])
-        tadd = carry()
-        if not last:
-            ac, as_ = arr[t]
-            cp = ("cp%d" % t, 32)
-            n = "H%d" % (t + 1)
-            z = mm(T.pa[:, 0:128], 128, "qr", 128 * (t + 1), M, 0, (ac, as_, cp, trc[t + 1], trs[t + 1], tsqa))
-            hc, hs = [], []
-            for h in range(2):
-                off = T.mrg[:, 16 * t + 8 * h:16 * t + 8 * h + 8]
-                hc.append(pick(n, M, 128 * h, 128 * h + 128, 0, W, off, (ac, cp, tm)))
-                hs.append(picks(n, M, 128 * h, 128 * h + 128, 0, W, off, (as_, cp, tm)))
-                score(t + 1, h)
-            tsqa = func(T.sqa[:], T.pa[:, 0:K], F.Square, z, tu)
+            z = copy(T.yb[0:32, :, 2 * a:2 * a + 2], T.YS[32 * a:32 * a + 32, 15:64:16], x)
+        if listed:
+            town = ts(T.own[:], T.YS[:, 15:64:16], float(K), None, A.add, None)
             if t + 2 < R:
-                query_codes(t + 2)
+                number(t)
+        elif not last:
+            staying(T.us, 0, uses[0], to[0])
+            tus = staying(T.us, 1, uses[1], to[1])
+        for a in range(4):
+            tm = ts(T.mrg[32 * a:32 * a + 32, 16 * t:16 * t + 16], T.yb[0:32, :, :], float(K), None, A.add, None, z)
+        if listed:
+            z, L = came("arl", t), T["L%d" % t][:]
+            store(z)
+            if t + 2 < R:
+                lay_beside("F%d" % (t + 2), 2 * K, "F%d" % t, 0, n, "cpf%d" % (t + 2), z, *far[t])
+            x = copy(T.US[:, 0:K], T.sqf[:, 0:n].indirect(L), z, tsqf)
+            arr[t] = (pick(M, 0, K, "F%d" % t, L), None)
+            y = copy(T.UD[:], T.US[:].indirect(T.own[:]), x, town)
+            half = [T.US[:].indirect(T.mrg[:, 16 * t + 8 * h:16 * t + 8 * h + 8]) for h in range(2)]
+            tu = [copy(T.U[:, u + P:u + P + 128], half[0], tm), func(T.U[:, u + P + 128:u + 2 * P], half[1], F.Copy, x, tm)]
+            arr[t] = (arr[t][0], picks(M, 0, K, "F%d" % t, L, z, *far[t]))
+            tv = [turn(T.UT[:], T.UD[:], y)] * 2
+            merge_codes(t, 0)
+        elif not last:
+            N, nxt = "F%d" % (t + 1), t + 1
+            left = ("H0", T.lst[:, 0:4]) if t == 1 else ("N2", T.lst[:, 8:12], ("cpn", 96))
+            x = pick(N, K, K, *left)
+            query_codes(t + 2)
+            ac, as_ = arr[t]
+            store(ac, as_)
+            send_columns(N, M, K, nxt, (ac,), (ac, as_))
+            if t == 1:
+                lay_beside("N2", 0, "M1", 0, K, "cpn")
+                lay_beside("N2", K, "M0", 0, K, "cpn", *arr[0])
+                lay_beside("N2", 2 * K, "H0", 0, P, "cpn")
+            z = mm(T.pa[:, 0:128], 128, "qr", 128 * (t + 1), M, 0, ac, as_, held(t), trc[t + 1], trs[t + 1], tsqa)
+            for h in range(2):
+                merge_codes(t, h)
+                merge_scales(t, h)
+                score(t + 1, h)
+            tsqa = func(T.US[:, 0:K], T.pa[:, 0:K], F.Square, z, *tu)
+            far[nxt] = (came("arc", nxt), came("ars", nxt), ("cpf%d" % nxt, 32), x, picks(N, K, K, *left))
+            if t + 3 < R:
+                query_codes(t + 3)
             use(t + 1, 0)
-            tu = copy(T.U[:, u + P:u + 2 * P].indirect(lst), T.sqa[:], tadd, tsqa)
+            tu = [copy(T.U[:, u + P:u + 2 * P].indirect(lst), T.US[:, 0:K], tadd, tsqa)] * 2
             use(t + 1, 1)
+            number(t)
         else:
             products(t, tm)
+            store()
 
     for q in ("v", "s", "p", "g"):
         wait("y", (own[q], count[q]))
-    wait("y", ("sty", 16 * R * O))
+    wait("y", ("sty", 16 * (R - 1) * O), ("end", 16 * O))
     wait("g", ("loc", sent[0]))

@@ -4,8 +4,9 @@ P, K, R, O = 256, 64, 6, 2
 PART = [1, 2, 1, 2, 1, 2]
 W = K + P
 QW = 32
-STAY = 1024.0
-FAR = 4096.0
+STAY = 2048.0
+FAR = 8192.0
+HALF = "float16"
 CODE, PLANE = "float8_e4m3fn_x4", "uint8"
 
 SCRATCH = {
@@ -28,18 +29,17 @@ SCRATCH = {
     "sqf": ("sbuf", [128, 2 * P], "float32"),
     "uc": ("sbuf", [128, 2], "float32"),
     "us": ("sbuf", [128, 2], "float32"),
-    "X": ("sbuf", [128, 640], "bfloat16"),
-    "G": ("sbuf", [128, 640], "bfloat16"),
-    "SO": ("sbuf", [128, 640], "bfloat16"),
+    "X": ("sbuf", [128, 2 * P], "bfloat16"),
+    "G": ("sbuf", [128, P], "bfloat16"),
+    "SO": ("sbuf", [128, 2 * P], HALF),
     "sgn": ("sbuf", [128, P], "bfloat16"),
-    "sa": ("sbuf", [128, 1], "float32"),
-    "Z": ("sbuf", [128, P], "bfloat16"),
-    "E": ("sbuf", [128, P], "bfloat16"),
-    "ET": ("sbuf", [128, 2 * P], "bfloat16"),
-    "ER": ("sbuf", [128, 2 * P], "bfloat16"),
-    "ES": ("sbuf", [128, 2 * P], "bfloat16"),
-    "fb": ("sbuf", [128, 4], "bfloat16"),
-    "num": ("sbuf", [128, 2 * (R - 1)], "bfloat16"),
+    "sa": ("sbuf", [128, 2], "float32"),
+    "Zb": ("sbuf", [128, 128], "bfloat16"),
+    "Z": ("sbuf", [128, 128], HALF),
+    "E": ("sbuf", [128, P], HALF),
+    "ET": ("sbuf", [128, 640], HALF),
+    "ES": ("sbuf", [128, 640], HALF),
+    "num": ("sbuf", [128, 2 * (R - 1)], HALF),
     "plk": ("sbuf", [128, 2], "float32"),
     "st": ("sbuf", [128, 2], "float32"),
     "sl": ("sbuf", [128, 2 * R], "float32"),
@@ -60,9 +60,9 @@ SCRATCH = {
     "pr": ("psum", [128, 1024], "float32"),
     "py": ("psum", [128, 512 * O], "float32"),
 }
-SEMAPHORES = ["sv", "ss", "sp", "sg", "ld0", "ld1", "ldq", "ldw", "loc", "sty", "end", "cpn"]
+SEMAPHORES = ["sv", "ss", "sp", "sg", "ld0", "ld1", "ldq", "ldw", "loc", "sty", "end", "cpn", "arh0"]
 for _t in range(R):
-    _stages = [("H", P), ("M", W), ("S", K) if _t % 2 else ("F", P + K * _t)]
+    _stages = [("M", W), ("S", K) if _t % 2 else ("F", P + K * _t)] + ([("H", P)] if _t % 2 or _t == 0 else [])
     for _n, _w in _stages:
         SCRATCH["%s%d" % (_n, _t)] = ("sbuf", [128, _w], CODE)
         SCRATCH["%s%ds" % (_n, _t)] = ("sbuf", [128, _w], PLANE)
@@ -122,7 +122,10 @@ def rank_program(g, core, T, topo):
         syn.dma_start(T[out + "s"][:, a:a + n], T[src + "s"][:, b:b + n]).then_inc(T.sem[sem], 16)
 
     def held(t):
-        return ("cp%d" % t, 64 if t % 2 and t < R - 1 else 32)
+        return ("cp%d" % t, 64 if t % 2 and t < R - 1 else 32) if t % 2 or t == 0 else None
+
+    def hold(t):
+        return ("H%d" % t, 0) if t % 2 or t == 0 else ("M%d" % t, K)
 
     def pick(out, a, n, win, off, *deps):
         wait("v", *deps)
@@ -170,6 +173,12 @@ def rank_program(g, core, T, topo):
         wait("s", *deps)
         return done("s", act.activation(out, in_, f))
 
+    def shift(q, out, in_, scale, bias, dep):
+        if q == "v":
+            return ts(out, in_, scale, bias, A.mult, A.add, dep)
+        wait("s", dep)
+        return done("s", act.activation(out, in_, F.Identity, bias=bias, scale=scale))
+
     def iota(out, pattern, base, step):
         return done("g", g.iota(out, pattern, base, step, allow_small_or_imprecise_dtypes=True))
 
@@ -182,21 +191,19 @@ def rank_program(g, core, T, topo):
     tiq = done("g", g.iota(T.iq[:], [[1, R], [0, 8]], 0, 0))
     tip = done("g", g.iota(T.ip[:], [[1, 1]], 0, 1))
     tj = iota(T.J[:], [[0, 2], [1, 16]], 0, 0)
+    iota(T.plk[:], [[P, 2]], 0, 2)
+    tz = iota(T.Zb[:], [[-32, 4], [0, 2], [-2, 16]], 128, 0)
     wait("g", tg1)
-    done("g", g.affine_select(T.G[:, 0:128], T.G[:, 0:128], [[-1, 128]], A.not_equal, 0.0, 0, 1))
-    tk = done("g", g.affine_select(T.G[:, 512:640], T.G[:, 512:640], [[-1, 128]], A.not_equal, -1.0, 0, 1))
-    iota(T.Z[:, 0:128], [[16, 4], [0, 2], [1, 16]], 0, 0)
-    iota(T.Z[:, 128:256], [[-32, 4], [0, 2], [-2, 16]], P, 0)
-    iota(T.num[:, 0:2], [[128, 2]], 0, 1)
-    tz = iota(T.plk[:], [[128, 2]], 0, 1)
+    tk = done("g", g.affine_select(T.G[:, 0:128], T.G[:, 0:128], [[-1, 128]], A.not_equal, -1.0, 0, 1))
+    ter = fill(T.YR[:], 0.0)
     toff = copy(T.offq[:], T.iq[:], tiq)
     ta = ts(T.ipm[:], T.ip[:], 15, None, A.bitwise_and, None, tip)
-    fill(T.YR[:], 0.0)
-    ter = fill(T.ER[:], 1.0)
+    ter = fill(T.YR[:, 0:64:16], -FAR, ter)
     ta = copy(T.idf[:], T.ipm[:], ta)
-    fill(T.G[:, 128:129], -1.0, ter)
-    fill(T.ER[:, 0:2 * P:2 * K], 0.0)
-    fill(T.YR[:, 0:64:16], -FAR)
+    copy(T.Z[:], T.Zb[:], tz)
+    x = ts(T.ET[0:64, 0:640:5], T.Zb[0:64, :], 0.0, None, A.mult, None)
+    copy(T.ET[32:64, 0:640:160], T.YR[32:64, 0:64:16], x, ter)
+    tz = ts(T.num[:, 0:2], T.plk[:], float(2 * P), None, A.add, None)
 
     trc, trs = [None] * R, [None] * R
 
@@ -207,39 +214,44 @@ def rank_program(g, core, T, topo):
         trs[t] = picks("qr", 128 * t, 128, "qk", T.offq[:, 8 * t:8 * t + 8], tq, toff)
 
     tq = quantize("qk", 0, 128, T.qin, ("ldq", 16), tq)
-    ta = ts(T.JG[:], T.J[:], T.idf[:], FAR + K, A.is_equal, A.mult, ta, tj)
-    query_codes(0)
+    ta = ts(T.JG[:], T.J[:], T.idf[:], FAR, A.is_equal, A.mult, ta, tj)
     query_scales(0)
     query_scales(1)
-    hc = [quantize("H0", 128 * h, 128, T.cin, ("ld%d" % h, 16)) for h in range(2)]
+    hc = [quantize("H0", 0, 128, T.cin, ("ld0", 16))]
+    query_codes(0)
+    hc.append(quantize("H0", 128, 128, T.cin, ("ld1", 16)))
     hs = list(hc)
-    send_columns("F0", "H0", P, 0, hc, hc)
+    send(u8(T.F0[:, 0:128]), u8(T.H0[:, 0:128]), "arh", 0, hc[0])
+    send(T.F0s[:], T.H0s[:], "ars", 0, hc[1])
+    send(u8(T.F0[:, 128:P]), u8(T.H0[:, 128:P]), "arc", 0)
     tu = []
+    tc = [mm(T.pc[:, 0:128], 128, "H0", 0, "qk", 0, hc[0], tq), None]
     for h in range(2):
         x = mm(T.pr[:, 512 * h:512 * h + 128], 128, "qr", 0, "H0", 128 * h, trc[0], trs[0], hc[h])
         tu.append(func(T.U[:, 128 * h:128 * h + 128], T.pr[:, 512 * h:512 * h + 128], F.Square, x))
 
     tm = tadd = tus = tsqa = tsqf = None
     tv = [None, None]
-    tc = [None, None]
     tyc = [None, None]
     tyw = [None, None]
-    tsq = tu[0]
+    tsq = list(tu)
+    tsn = [None, None]
     tnum = [None] * R
     arr = [(came("arc", t), came("ars", t)) for t in range(R)]
-    far = {0: arr[0]}
-    order = [T.SO[:, 383:384], T.SO[:, 639:640]]
+    far = {0: arr[0] + (came("arh", 0),)}
+    order = [T.SO[:, P * h + P - 1:P * h + P] for h in range(2)]
     stores = []
 
-    def products(t, tm):
+    def products(t, tm, tiles=range(O - 1, -1, -1), between=lambda: None):
         tail = t == R - 1
         z = {}
-        for o in range(O - 1, -1, -1):
+        for o in tiles:
             z[o] = mm(T.py[:, 512 * o:512 * o + 128], 128, "wk", 128 * o, "M%d" % t, 0, tw, arr[t][0], arr[t][1], held(t), tyc[o])
         for o in z:
             b = (t * O + o) * W
             src = T.py[:, 512 * o:512 * o + K]
             tyc[o] = copy(T.yw[:, b:b + K], src, z[o]) if tail else func(T.yw[:, b:b + K], src, F.Copy, z[o])
+        between()
         for o in z:
             b = (t * O + o) * W
             n = b + O * W + K
@@ -257,12 +269,13 @@ def rank_program(g, core, T, topo):
             wait(q, x, *deps)
             queue[q].dma_start(T.y[:, a:a + P], T.yw[:, n:n + P]).then_inc(T.sem[sem], 16)
 
-    def ahead(t, *deps):
-        x = mm(T.pr[:, 0:P], P, "qr", 128 * t, "H%d" % (t - 1), 0, trc[t], trs[t], tsq, hc[1], hs[1])
-        return func(T.sqn[:], T.pr[:, 0:P], F.Square, x, *deps)
+    def ahead(t, h):
+        bank = T.pr[:, 512 * h:512 * h + 128]
+        x = mm(bank, 128, "qr", 128 * t, hold(t - 1)[0], hold(t - 1)[1] + 128 * h, trc[t], trs[t], tsq[h], hc[h], hs[h])
+        tsq[h] = tsn[h] = func(T.sqn[:, 128 * h:128 * h + 128], bank, F.Square, x, tadd)
 
     def score(t, h):
-        tc[h] = mm(T.pc[:, 512 * h:512 * h + 128], 128, "H%d" % t, 128 * h, "qk", 0, hc[h], hs[h], tq, tv[h])
+        tc[h] = mm(T.pc[:, 512 * h:512 * h + 128], 128, hold(t)[0], hold(t)[1] + 128 * h, "qk", 0, hc[h], hs[h], tq, tv[h])
 
     def use(t, h):
         s = T.pc[:, 512 * h + t:512 * h + t + 1]
@@ -271,169 +284,173 @@ def rank_program(g, core, T, topo):
         else:
             tv[h] = ts(T.uc[:, h:h + 1], s, s, None, A.mult, None, tc[h])
 
-    def staying(out, h, x, to):
-        return ts(out[:, h:h + 1], order[h], float((K, P - 2 * K)[h]), x, (A.is_ge, A.is_le)[h], A.mult, to)
+    def keep(h, x):
+        return ts(T.us[:, h:h + 1], order[h], 0.0, x, A.is_le, A.mult)
 
     def mark(t, h, to):
         c = h if t % 2 else 2 * t + h
-        return ts(T.E[:, 128 * h:128 * h + 128], T.Z[:, 128 * h:128 * h + 128], order[h], T.num[:, c:c + 1], A.is_equal, A.mult, to, tz, tnum[t])
+        return ts(T.E[:, 128 * h:128 * h + 128], T.Z[:], order[h], T.num[:, c:c + 1], A.is_equal, A.mult, to, tz, tnum[t])
 
-    def slot(t, h, x):
-        if h:
-            return ts(T.sl[:, 2 * t + 1:2 * t + 2], order[1], -0.5, T.st[:, 1:2], A.mult, A.add, x)
-        return ts(T.sl[:, 2 * t:2 * t + 1], order[0], T.st[:, 0:1], -128.0, A.add, A.add, x)
+    def slot(t, x):
+        return tt(T.sl[:, 2 * t:2 * t + 2], T.st[:], T.SO[:, P - 1:2 * P:P], A.subtract, x)
 
     def lay(t, h, x):
         return ts(T.Y[:, 32 * h:32 * h + 32], T.JG[:], T.sl[:, 2 * t + h:2 * t + h + 1], T.plk[:, h:h + 1], A.add, A.min, x)
 
-    def number(t, *deps):
+    def number(t):
         for h in range(2):
             c = 2 * t + h
-            tnum[t + 1] = ts(T.num[:, c + 2:c + 3], T.sl[:, c:c + 1], float(128 - K * (t + 1)), T.num[:, c:c + 1], A.add, A.min, *deps)
-        return tnum[t + 1]
+            tnum[t + 1] = ts(T.num[:, c + 2:c + 3], T.sl[:, c:c + 1], float(2 * P - 2 * K * t), T.num[:, c:c + 1], A.add, A.min)
 
-    def merge_codes(t, h):
-        hc[h] = pick("H%d" % (t + 1), 128 * h, 128, "M%d" % t, T.mrg[:, 16 * t + 8 * h:16 * t + 8 * h + 8], arr[t][0], held(t), tm)
+    def merge_codes(t, a, n):
+        hc[a // 128] = pick(hold(t + 1)[0], hold(t + 1)[1] + a, n, "M%d" % t, T.mrg[:, 16 * t + a // 16:16 * t + (a + n) // 16], arr[t][0], held(t), tm)
 
-    def merge_scales(t, h):
-        hs[h] = picks("H%d" % (t + 1), 128 * h, 128, "M%d" % t, T.mrg[:, 16 * t + 8 * h:16 * t + 8 * h + 8], arr[t][1], held(t), tm)
+    def merge_scales(t, a, n):
+        hs[a // 128] = picks(hold(t + 1)[0], hold(t + 1)[1] + a, n, "M%d" % t, T.mrg[:, 16 * t + a // 16:16 * t + (a + n) // 16], arr[t][1], held(t), tm)
 
-    for h in range(2):
-        score(0, h)
+    score(0, 1)
     tcon = ts(T.JG[:], T.JG[:], -FAR, None, A.add, None, ta)
     query_codes(1)
-    query_codes(2)
+    use(0, 0)
     tw = quantize("wk", 0, 128 * O, T.win, ("ldw", 16))
-    for h in range(2):
-        use(0, h)
+    query_codes(2)
+    use(0, 1)
 
     for t in range(R):
         H, M, u = "H%d" % t, "M%d" % t, t * P
         last, listed = t == R - 1, t % 2 == 0
-        if listed:
+        if t == 0:
             lay_beside(M, K, H, 0, P, "cp%d" % t, hc[1], hs[1])
         uses = [T.uc[:, h:h + 1] if listed else T.UT[:, 32 * h:32 * h + 1] for h in range(2)]
-        wait("s", tv[1], *tu)
-        z = done("s", act.activation(T.sgn[:], T.U[:, u:u + P], F.Sign, bias=uses[1], scale=-1.0, accum_out=T.sa[:]))
-        ts(T.X[:, 0:128], T.U[:, u:u + 128], uses[0], None, A.is_equal, None, tv[0], tu[0])
-        ts(T.X[:, 128:256], T.U[:, u:u + 128], uses[0], None, A.is_le, None)
-        x0 = ts(T.X[:, 256:384], T.U[:, u + 128:u + 256], uses[0], None, A.is_lt, None, tu[1])
-        x1 = ts(T.X[:, 384:640], T.U[:, u:u + 256], uses[1], None, A.is_equal, None, tv[1])
-        to = [scan(T.SO[:, 0:384], T.G[:, 0:384], T.X[:, 0:384], 0.0, A.mult, A.add, x0, tk, tcon),
-              scan(T.SO[:, 384:640], T.G[:, 384:640], T.X[:, 384:640], T.sa[:], A.mult, A.add, x1, z)]
-        if not listed:
-            merge_scales(t - 1, 0)
+        z, x = [], []
+        for h in range(2):
+            mine, other = T.U[:, u + 128 * h:u + 128 * h + 128], T.U[:, u + 128 - 128 * h:u + P - 128 * h]
+            ready = tu if t else tu[h:h + 1]
+            wait("s", tv[h], *ready)
+            z.append(done("s", act.activation(T.sgn[:, 128 * h:128 * h + 128], mine, F.Sign, bias=uses[h], scale=-1.0, accum_out=T.sa[:, h:h + 1])))
+            ts(T.X[:, P * h:P * h + 128], mine, uses[h], None, A.is_equal, None, tv[h], *ready)
+            x.append(ts(T.X[:, P * h + 128:P * h + P], other, uses[h], -2.0, (A.is_lt, A.is_le)[h], A.mult, tu[1 - h]))
+        to = [scan(T.SO[:, P * h:P * h + P], T.G[:], T.X[:, P * h:P * h + P], T.sa[:, h:h + 1], A.mult, A.add, x[h], z[h], tk, tcon) for h in range(2)]
+        if listed:
+            ahead(t + 1, 0)
+            if t:
+                products(t - 1, tm, [1], lambda: ahead(t + 1, 1))
+            else:
+                ahead(t + 1, 1)
+        else:
+            merge_scales(t - 1, 0, 128)
             lay_beside(M, K, H, 0, K if last else 128, "cp%d" % t, hc[0], hs[0])
+            if last:
+                products(t - 1, tm)
+                store()
+            merge_scales(t - 1, 128, K)
+            merge_scales(t - 1, 128 + K, K)
             if not last:
-                merge_scales(t - 1, 1)
-        if t:
-            products(t - 1, tm)
-        if last:
-            store()
-            merge_scales(t - 1, 1)
+                products(t - 1, tm, [1], lambda: ahead(t + 1, 0))
         e0 = mark(t, 0, to[0])
-        s0 = staying(T.st, 0, STAY, to[0])
+        if not listed:
+            merge_codes(t - 1, 128, K)
         e1 = mark(t, 1, to[1])
-        s1 = staying(T.st, 1, STAY, to[1])
+        s1 = ts(T.st[:], T.SO[:, P - 1:2 * P:P], 0.0, STAY, A.is_le, A.mult)
         for h, e in enumerate((e0, e1)):
             for a in range(2):
-                x = turn(T.ET[0:64, 2 * h + a:2 * P:4], T.E[64 * a:64 * a + 64, 128 * h:128 * h + 128], e)
-        if listed:
-            s0 = slot(t, 0, s0)
-            s1 = slot(t, 1, s1)
-        else:
-            merge_codes(t - 1, 1)
+                x = turn(T.ET[0:64, 1 + 2 * h + a:640:5], T.E[64 * a:64 * a + 64, 128 * h:128 * h + 128], e)
+        s1 = slot(t, s1)
+        if not listed:
+            merge_codes(t - 1, 128 + K, K)
             if not last:
                 lay_beside(M, K + 128, H, 128, 128, "cp%d" % t, hc[1], hs[1])
-        if not last:
-            tsq = ahead(t + 1, tadd)
         if t == 0:
             for o in range(O):
                 z = mm(T.py[:, 512 * o:512 * o + P], P, "wk", 128 * o, "H0", 0, tw)
                 tyw[o] = tyc[o] = func(T.yw[:, o * W + K:o * W + W], T.py[:, 512 * o:512 * o + P], F.Copy, z)
-        x = scan(T.ES[0:64, :], T.ER[0:64, :], T.ET[0:64, :], 0.0, A.mult, A.add, x)
-        if listed:
-            s0 = lay(t, 0, s0)
-            s1 = lay(t, 1, s1)
-        else:
-            s0 = slot(t, 0, s0)
-            s1 = slot(t, 1, s1)
-        x = tt(T.fb[0:32, :], T.ES[0:32, 127:2 * P:128], T.ES[32:64, 127:2 * P:128], A.add, x)
+        x = scan(T.ES[0:32, :], T.ET[0:32, :], T.ET[32:64, :], 0.0, A.max, A.add, x)
         lst = T.lst[:, 4 * t:4 * t + 4]
-        for a in range(4):
-            tl = ts(T.lst[32 * a:32 * a + 32, 4 * t:4 * t + 4], T.fb[0:32, :], float(K * t if listed else 0), None, A.add, None, x)
+        tl = [shift(q, T.lst[32 * a:32 * a + 32, 4 * t:4 * t + 4], T.ES[0:32, 159:640:160], 0.5, float((K * t if listed else 0) - P), x) for a, q in enumerate("vvvs")]
+        lay(t, 0, s1)
+        s1 = lay(t, 1, s1)
         if listed:
-            send(T["L%d" % t][:], lst, "arl", t, tl)
+            send(T["L%d" % t][:], lst, "arl", t, *tl)
             n = P + K * t
-            x = mm(T.pa[:, 0:n], n, "qr", 128 * (t + 1), "F%d" % t, 0, trc[t + 1], trs[t + 1], tsqa, *far[t])
-            tsqa = tsqf = func(T.sqf[:, 0:n], T.pa[:, 0:n], F.Square, x)
+            if t:
+                x = mm(T.pa[:, 0:n], n, "qr", 128 * (t + 1), "F%d" % t, 0, trc[t + 1], trs[t + 1], tsqa, *far[t])
+                tsqa = tsqf = func(T.sqf[:, 0:n], T.pa[:, 0:n], F.Square, x)
+                products(t - 1, tm, [0])
+            else:
+                for h, bank in enumerate((T.pr[:, 512:640], T.pa[:, 0:128])):
+                    x = mm(bank, 128, "qr", 128, "F0", 128 * h, trc[1], trs[1], far[0][1], far[0][2 - 2 * h], tsq[1])
+                    tsqa = tsqf = func(T.sqf[:, 128 * h:128 * h + 128], bank, F.Square, x)
+                tsq[1] = tsqf
         else:
-            s0 = lay(t, 0, s0)
-            s1 = lay(t, 1, s1)
             S = "S%d" % t
-            send_columns(M, S, K, t, (pick(S, 0, K, H, lst, tl),), (picks(S, 0, K, H, lst, tl, hs[1]),))
+            send_columns(M, S, K, t, (pick(S, 0, K, H, lst, *tl),), (picks(S, 0, K, H, lst, hs[1], *tl),))
+            if not last:
+                ahead(t + 1, 1)
+                products(t - 1, tm, [0])
         if t + 2 < R:
             query_scales(t + 2)
         todo = [] if last else [0, 1]
 
         def carry():
             if todo:
-                a = 128 * todo.pop(0)
+                h = todo.pop(0)
+                a = 128 * h
                 out = T.US[:, K + a:K + a + 128] if listed else T.U[:, u + P + a:u + P + a + 128]
-                return tt(out, T.U[:, u + a:u + a + 128], T.sqn[:, a:a + 128], A.add, tsq, *tu)
+                return tt(out, T.U[:, u + a:u + a + 128], T.sqn[:, a:a + 128], A.add, tsn[h], *tu)
             return tadd
 
-        x = turn(T.YT[:], T.Y[:], s1)
-        carry()
-        x = scan(T.YS[:], T.YR[:], T.YT[:], 0.0, A.add, A.max, x)
-        tadd = carry()
-        for a in range(4):
-            z = copy(T.yb[0:32, :, 2 * a:2 * a + 2], T.YS[32 * a:32 * a + 32, 15:64:16], x)
         if listed:
-            town = ts(T.own[:], T.YS[:, 15:64:16], float(K), None, A.add, None)
+            carry()
+        x = turn(T.YT[:], T.Y[:], s1)
+        tadd = carry()
+        x = scan(T.YS[:], T.YR[:], T.YT[:], 0.0, A.add, A.max, x)
+        if listed:
             if t + 2 < R:
                 number(t)
         elif not last:
-            staying(T.us, 0, uses[0], to[0])
-            tus = staying(T.us, 1, uses[1], to[1])
+            keep(0, uses[0])
+            tus = keep(1, uses[1])
         for a in range(4):
-            tm = ts(T.mrg[32 * a:32 * a + 32, 16 * t:16 * t + 16], T.yb[0:32, :, :], float(K), None, A.add, None, z)
+            z = copy(T.yb[0:32, :, 2 * a:2 * a + 2], T.YS[32 * a:32 * a + 32, 15:64:16], x)
+        if listed:
+            town = ts(T.own[:], T.YS[:, 15:64:16], 0.5, float(K), A.mult, A.add)
+        tadd = carry()
+        for a in range(4):
+            tm = ts(T.mrg[32 * a:32 * a + 32, 16 * t:16 * t + 16], T.yb[0:32, :, :], 0.5, float(K), A.mult, A.add, z)
         if listed:
             z, L = came("arl", t), T["L%d" % t][:]
             store(z)
-            if t + 2 < R:
-                lay_beside("F%d" % (t + 2), 2 * K, "F%d" % t, 0, n, "cpf%d" % (t + 2), z, *far[t])
             x = copy(T.US[:, 0:K], T.sqf[:, 0:n].indirect(L), z, tsqf)
             arr[t] = (pick(M, 0, K, "F%d" % t, L), None)
             y = copy(T.UD[:], T.US[:].indirect(T.own[:]), x, town)
-            half = [T.US[:].indirect(T.mrg[:, 16 * t + 8 * h:16 * t + 8 * h + 8]) for h in range(2)]
-            tu = [copy(T.U[:, u + P:u + P + 128], half[0], tm), func(T.U[:, u + P + 128:u + 2 * P], half[1], F.Copy, x, tm)]
+            tu = [copy(T.U[:, u + P:u + P + K], T.US[:].indirect(T.mrg[:, 16 * t:16 * t + 4]), tm),
+                  func(T.U[:, u + P + K:u + 2 * P], T.US[:].indirect(T.mrg[:, 16 * t + 4:16 * t + 16]), F.Copy, x, tm)]
             arr[t] = (arr[t][0], picks(M, 0, K, "F%d" % t, L, z, *far[t]))
             tv = [turn(T.UT[:], T.UD[:], y)] * 2
-            merge_codes(t, 0)
+            merge_codes(t, 0, 128)
+            if t == 0:
+                lay_beside("N2", K, "M0", 0, W, "cpn", held(0), *arr[0])
         elif not last:
             N, nxt = "F%d" % (t + 1), t + 1
-            left = ("H0", T.lst[:, 0:4]) if t == 1 else ("N2", T.lst[:, 8:12], ("cpn", 96))
+            left = ("H0", T.lst[:, 0:4]) if t == 1 else ("N2", T.lst[:, 8:12], ("cpn", 64))
             x = pick(N, K, K, *left)
-            query_codes(t + 2)
+            for i in range(t + 2, min(t + 4, R)):
+                query_codes(i)
             ac, as_ = arr[t]
-            store(ac, as_)
             send_columns(N, M, K, nxt, (ac,), (ac, as_))
+            lay_beside(N, 2 * K, "F%d" % (t - 1), 0, P + K * (t - 1), "cpf%d" % nxt, ac, as_, *far[t - 1])
+            store()
             if t == 1:
                 lay_beside("N2", 0, "M1", 0, K, "cpn")
-                lay_beside("N2", K, "M0", 0, K, "cpn", *arr[0])
-                lay_beside("N2", 2 * K, "H0", 0, P, "cpn")
             z = mm(T.pa[:, 0:128], 128, "qr", 128 * (t + 1), M, 0, ac, as_, held(t), trc[t + 1], trs[t + 1], tsqa)
             for h in range(2):
-                merge_codes(t, h)
-                merge_scales(t, h)
+                merge_codes(t, 128 * h, 128)
+                merge_scales(t, 128 * h, 128)
                 score(t + 1, h)
             tsqa = func(T.US[:, 0:K], T.pa[:, 0:K], F.Square, z, *tu)
             far[nxt] = (came("arc", nxt), came("ars", nxt), ("cpf%d" % nxt, 32), x, picks(N, K, K, *left))
-            if t + 3 < R:
-                query_codes(t + 3)
-            use(t + 1, 0)
             tu = [copy(T.U[:, u + P:u + 2 * P].indirect(lst), T.US[:, 0:K], tadd, tsqa)] * 2
+            use(t + 1, 0)
             use(t + 1, 1)
             number(t)
         else:

from concourse.mybir import dt, AluOpType, ActivationFunctionType

P, K, R, O = 256, 64, 6, 2
PART = [1, 2, 1, 2, 1, 2]
W = K + P
QW = 32
STAY = 2048.0
FAR = 8192.0
HALF = "float16"
CODE, PLANE = "float8_e4m3fn_x4", "uint8"

SCRATCH = {
    "cin": ("sbuf", [128, 4 * P], "bfloat16"),
    "qin": ("sbuf", [128, 512], "bfloat16"),
    "win": ("sbuf", [128, 512 * O], "bfloat16"),
    "qk": ("sbuf", [128, 128], CODE), "qks": ("sbuf", [128, 128], PLANE),
    "qr": ("sbuf", [128, 128 * R], CODE), "qrs": ("sbuf", [128, 128 * R], PLANE),
    "wk": ("sbuf", [128, 128 * O], CODE), "wks": ("sbuf", [128, 128 * O], PLANE),
    "N2": ("sbuf", [128, P + 2 * K], CODE), "N2s": ("sbuf", [128, P + 2 * K], PLANE),
    "offq": ("sbuf", [128, 8 * R], "uint16"),
    "lst": ("sbuf", [128, R * K // 16], "uint16"),
    "mrg": ("sbuf", [128, R * P // 16], "uint16"),
    "own": ("sbuf", [128, 4], "uint16"),
    "U": ("sbuf", [128, R * P], "float32"),
    "US": ("sbuf", [128, W], "float32"),
    "UD": ("sbuf", [128, K], "float32"),
    "UT": ("sbuf", [128, K], "float32"),
    "sqn": ("sbuf", [128, P], "float32"),
    "sqf": ("sbuf", [128, 2 * P], "float32"),
    "uc": ("sbuf", [128, 2], "float32"),
    "us": ("sbuf", [128, 2], "float32"),
    "X": ("sbuf", [128, 2 * P], "bfloat16"),
    "G": ("sbuf", [128, P], "bfloat16"),
    "SO": ("sbuf", [128, 2 * P], HALF),
    "sgn": ("sbuf", [128, P], "bfloat16"),
    "sa": ("sbuf", [128, 2], "float32"),
    "Zb": ("sbuf", [128, 128], "bfloat16"),
    "Z": ("sbuf", [128, 128], HALF),
    "E": ("sbuf", [128, P], HALF),
    "ET": ("sbuf", [128, 640], HALF),
    "ES": ("sbuf", [128, 640], HALF),
    "num": ("sbuf", [128, 2 * (R - 1)], HALF),
    "plk": ("sbuf", [128, 2], "float32"),
    "st": ("sbuf", [128, 2], "float32"),
    "sl": ("sbuf", [128, 2 * R], "float32"),
    "J": ("sbuf", [128, 32], "bfloat16"),
    "JG": ("sbuf", [128, 32], "bfloat16"),
    "Y": ("sbuf", [128, 64], "bfloat16"),
    "YT": ("sbuf", [128, 64], "bfloat16"),
    "YR": ("sbuf", [128, 64], "bfloat16"),
    "YS": ("sbuf", [128, 64], "bfloat16"),
    "yb": ("sbuf", [128, 2, 8], "bfloat16"),
    "iq": ("sbuf", [128, 8 * R], "int32"),
    "ip": ("sbuf", [128, 1], "int32"),
    "ipm": ("sbuf", [128, 1], "int32"),
    "idf": ("sbuf", [128, 1], "float32"),
    "yw": ("sbuf", [128, (R + 1) * O * W], "float32"),
    "pc": ("psum", [128, 1024], "float32"),
    "pa": ("psum", [128, 512], "float32"),
    "pr": ("psum", [128, 1024], "float32"),
    "py": ("psum", [128, 512 * O], "float32"),
}
SEMAPHORES = ["sv", "ss", "sp", "sg", "ld0", "ld1", "ldq", "ldw", "loc", "sty", "end", "cpn", "arh0"]
for _t in range(R):
    _stages = [("M", W), ("S", K) if _t % 2 else ("F", P + K * _t)] + ([("H", P)] if _t % 2 or _t == 0 else [])
    for _n, _w in _stages:
        SCRATCH["%s%d" % (_n, _t)] = ("sbuf", [128, _w], CODE)
        SCRATCH["%s%ds" % (_n, _t)] = ("sbuf", [128, _w], PLANE)
    SEMAPHORES += [_n + str(_t) for _n in ("cp", "arc", "ars")]
    if _t % 2 == 0:
        SCRATCH["L%d" % _t] = ("sbuf", [128, K // 16], "uint16")
        SEMAPHORES += [_n + str(_t) for _n in ("arl", "cpf")]


def rank_program(g, core, T, topo):
    rank = T.rank_of(core)
    if rank is None:
        return
    A, F = AluOpType, ActivationFunctionType
    vec, act, ten, syn = g.vector, g.scalar, g.tensor, g.sync
    queue = {"v": vec, "s": act, "p": ten, "g": g, "y": syn}
    count = {"v": 0, "s": 0, "p": 0, "g": 0}
    own = {"v": "sv", "s": "ss", "p": "sp", "g": "sg"}
    seen = {}
    sent = [0]

    def wait(q, *deps):
        top = {}
        for d in deps:
            if d is not None:
                top[d[0]] = max(top.get(d[0], 0), d[1])
        for s in top:
            if seen.get((q, s), 0) < top[s]:
                queue[q].wait_ge(T.sem[s], top[s])
                seen[(q, s)] = top[s]

    def done(q, ins):
        count[q] += 1
        ins.then_inc(T.sem[own[q]], 1)
        return (own[q], count[q])

    def u8(v):
        return v.bitcast(dt.uint8)

    def send(out_ap, in_ap, sem, t, *deps):
        wait("g", *deps)
        dst = T.cores[rank ^ PART[t]]
        rid, pid = topo.addr(dst)[:2]
        g.remote_dma(out_ap=out_ap, in_ap=in_ap, remote_sem=T.sem[sem + str(t)], local_sem=T.sem["loc"], pid=pid, routing_id=rid, dma_engine_mask=topo.mask(core, dst))
        sent[0] += len(topo.engines(core, dst))

    def send_columns(out, src, n, t, codes, scales):
        send(T[out + "s"][:, 0:n], T[src + "s"][:, 0:n], "ars", t, *scales)
        send(u8(T[out][:, 0:n]), u8(T[src][:, 0:n]), "arc", t, *codes)

    def came(sem, t):
        return (sem + str(t), len(topo.engines(T.cores[rank ^ PART[t]], core)))

    def lay_beside(out, a, src, b, n, sem, *deps):
        wait("y", *deps)
        syn.dma_start(u8(T[out][:, a:a + n]), u8(T[src][:, b:b + n])).then_inc(T.sem[sem], 16)
        syn.dma_start(T[out + "s"][:, a:a + n], T[src + "s"][:, b:b + n]).then_inc(T.sem[sem], 16)

    def held(t):
        return ("cp%d" % t, 64 if t % 2 and t < R - 1 else 32) if t % 2 or t == 0 else None

    def hold(t):
        return ("H%d" % t, 0) if t % 2 or t == 0 else ("M%d" % t, K)

    def pick(out, a, n, win, off, *deps):
        wait("v", *deps)
        return done("v", vec.tensor_copy(T[out][:, a:a + n].bitcast(dt.uint32), T[win][:].bitcast(dt.uint32).indirect(off)))

    def picks(out, a, n, win, off, *deps):
        wait("s", *deps)
        return done("s", act.activation(T[out + "s"][:, a:a + n], T[win + "s"][:].indirect(off), F.Copy))

    def mm(out, n, st, a, mv, b, *deps):
        wait("p", *deps)
        return done("p", ten.matmul_mx(out, T[st][:, a:a + 128], T[st + "s"][:, a:a + 128], T[mv][:, b:b + n], T[mv + "s"][:, b:b + n], True, True))

    def fill(ap, x, *deps):
        wait("v", *deps)
        return done("v", vec.memset(ap, x))

    def ts(out, in0, s1, s2, op0, op1, *deps):
        wait("v", *deps)
        if op1 is None:
            return done("v", vec.tensor_scalar(out, in0, s1, None, op0))
        return done("v", vec.tensor_scalar(out, in0, s1, s2, op0, op1))

    def tt(out, in0, in1, op, *deps):
        wait("v", *deps)
        return done("v", vec.tensor_tensor(out, in0, in1, op))

    def scan(out, d0, d1, first, op0, op1, *deps):
        wait("v", *deps)
        return done("v", vec.tensor_tensor_scan(out, d0, d1, first, op0, op1))

    def turn(out, in_, *deps):
        wait("v", *deps)
        return done("v", vec.transpose(out, in_))

    def copy(out, in_, *deps):
        wait("v", *deps)
        return done("v", vec.tensor_copy(out, in_))

    def quantize(out, a, n, src, *deps):
        wait("v", *deps)
        return done("v", vec.quantize_mx(T[out][:, a:a + n], T[out + "s"][:, a:a + n], src[:, 4 * a:4 * a + 4 * n]))

    def func(out, in_, f, *deps):
        wait("s", *deps)
        return done("s", act.activation(out, in_, f))

    def shift(q, out, in_, scale, bias, dep):
        if q == "v":
            return ts(out, in_, scale, bias, A.mult, A.add, dep)
        wait("s", dep)
        return done("s", act.activation(out, in_, F.Identity, bias=bias, scale=scale))

    def iota(out, pattern, base, step):
        return done("g", g.iota(out, pattern, base, step, allow_small_or_imprecise_dtypes=True))

    act.dma_start(T.qin[:, 0:QW], T.qt[:, 0:QW]).then_inc(T.sem.ldq, 16)
    for h in range(2):
        syn.dma_start(T.cin[:, 512 * h:512 * h + 512], T.c[:, 512 * h:512 * h + 512]).then_inc(T.sem["ld%d" % h], 16)
    syn.dma_start(T.win[:], T.w[:]).then_inc(T.sem.ldw, 16)
    tq = fill(T.qin[:, QW:512], 0.0)
    tg1 = fill(T.G[:], 1.0)
    tiq = done("g", g.iota(T.iq[:], [[1, R], [0, 8]], 0, 0))
    tip = done("g", g.iota(T.ip[:], [[1, 1]], 0, 1))
    tj = iota(T.J[:], [[0, 2], [1, 16]], 0, 0)
    iota(T.plk[:], [[P, 2]], 0, 2)
    tz = iota(T.Zb[:], [[-32, 4], [0, 2], [-2, 16]], 128, 0)
    wait("g", tg1)
    tk = done("g", g.affine_select(T.G[:, 0:128], T.G[:, 0:128], [[-1, 128]], A.not_equal, -1.0, 0, 1))
    ter = fill(T.YR[:], 0.0)
    toff = copy(T.offq[:], T.iq[:], tiq)
    ta = ts(T.ipm[:], T.ip[:], 15, None, A.bitwise_and, None, tip)
    ter = fill(T.YR[:, 0:64:16], -FAR, ter)
    ta = copy(T.idf[:], T.ipm[:], ta)
    copy(T.Z[:], T.Zb[:], tz)
    x = ts(T.ET[0:64, 0:640:5], T.Zb[0:64, :], 0.0, None, A.mult, None)
    copy(T.ET[32:64, 0:640:160], T.YR[32:64, 0:64:16], x, ter)
    tz = ts(T.num[:, 0:2], T.plk[:], float(2 * P), None, A.add, None)

    trc, trs = [None] * R, [None] * R

    def query_codes(t):
        trc[t] = pick("qr", 128 * t, 128, "qk", T.offq[:, 8 * t:8 * t + 8], tq, toff)

    def query_scales(t):
        trs[t] = picks("qr", 128 * t, 128, "qk", T.offq[:, 8 * t:8 * t + 8], tq, toff)

    tq = quantize("qk", 0, 128, T.qin, ("ldq", 16), tq)
    ta = ts(T.JG[:], T.J[:], T.idf[:], FAR, A.is_equal, A.mult, ta, tj)
    query_scales(0)
    query_scales(1)
    hc = [quantize("H0", 0, 128, T.cin, ("ld0", 16))]
    query_codes(0)
    hc.append(quantize("H0", 128, 128, T.cin, ("ld1", 16)))
    hs = list(hc)
    send(u8(T.F0[:, 0:128]), u8(T.H0[:, 0:128]), "arh", 0, hc[0])
    send(T.F0s[:], T.H0s[:], "ars", 0, hc[1])
    send(u8(T.F0[:, 128:P]), u8(T.H0[:, 128:P]), "arc", 0)
    tu = []
    tc = [mm(T.pc[:, 0:128], 128, "H0", 0, "qk", 0, hc[0], tq), None]
    for h in range(2):
        x = mm(T.pr[:, 512 * h:512 * h + 128], 128, "qr", 0, "H0", 128 * h, trc[0], trs[0], hc[h])
        tu.append(func(T.U[:, 128 * h:128 * h + 128], T.pr[:, 512 * h:512 * h + 128], F.Square, x))

    tm = tadd = tus = tsqa = tsqf = None
    tv = [None, None]
    tyc = [None, None]
    tyw = [None, None]
    tsq = list(tu)
    tsn = [None, None]
    tnum = [None] * R
    arr = [(came("arc", t), came("ars", t)) for t in range(R)]
    far = {0: arr[0] + (came("arh", 0),)}
    order = [T.SO[:, P * h + P - 1:P * h + P] for h in range(2)]
    stores = []

    def products(t, tm, tiles=range(O - 1, -1, -1), between=lambda: None):
        tail = t == R - 1
        z = {}
        for o in tiles:
            z[o] = mm(T.py[:, 512 * o:512 * o + 128], 128, "wk", 128 * o, "M%d" % t, 0, tw, arr[t][0], arr[t][1], held(t), tyc[o])
        for o in z:
            b = (t * O + o) * W
            src = T.py[:, 512 * o:512 * o + K]
            tyc[o] = copy(T.yw[:, b:b + K], src, z[o]) if tail else func(T.yw[:, b:b + K], src, F.Copy, z[o])
        between()
        for o in z:
            b = (t * O + o) * W
            n = b + O * W + K
            if tail and o == 0:
                n = b + K
                x = copy(T.yw[:, n:n + P].indirect(T.lst[:, 4 * t:4 * t + 4]), T.yw[:, b:b + K], tyc[o], ("sty", 16 * t * O))
            else:
                x = func(T.yw[:, n:n + P], T.yw[:, b:b + W].indirect(T.mrg[:, 16 * t:16 * t + 16]), F.Copy, tyc[o], tyw[o], tm)
            tyw[o] = x
            stores.append(("s" if tail and o == 1 else "y", (t * O + o) * P, n, x, "end" if tail else "sty"))

    def store(*deps):
        while stores:
            q, a, n, x, sem = stores.pop(0)
            wait(q, x, *deps)
            queue[q].dma_start(T.y[:, a:a + P], T.yw[:, n:n + P]).then_inc(T.sem[sem], 16)

    def ahead(t, h):
        bank = T.pr[:, 512 * h:512 * h + 128]
        x = mm(bank, 128, "qr", 128 * t, hold(t - 1)[0], hold(t - 1)[1] + 128 * h, trc[t], trs[t], tsq[h], hc[h], hs[h])
        tsq[h] = tsn[h] = func(T.sqn[:, 128 * h:128 * h + 128], bank, F.Square, x, tadd)

    def score(t, h):
        tc[h] = mm(T.pc[:, 512 * h:512 * h + 128], 128, hold(t)[0], hold(t)[1] + 128 * h, "qk", 0, hc[h], hs[h], tq, tv[h])

    def use(t, h):
        s = T.pc[:, 512 * h + t:512 * h + t + 1]
        if t:
            tv[h] = ts(T.uc[:, h:h + 1], s, s, T.us[:, h:h + 1], A.mult, A.add, tc[h], tus)
        else:
            tv[h] = ts(T.uc[:, h:h + 1], s, s, None, A.mult, None, tc[h])

    def keep(h, x):
        return ts(T.us[:, h:h + 1], order[h], 0.0, x, A.is_le, A.mult)

    def mark(t, h, to):
        c = h if t % 2 else 2 * t + h
        return ts(T.E[:, 128 * h:128 * h + 128], T.Z[:], order[h], T.num[:, c:c + 1], A.is_equal, A.mult, to, tz, tnum[t])

    def slot(t, x):
        return tt(T.sl[:, 2 * t:2 * t + 2], T.st[:], T.SO[:, P - 1:2 * P:P], A.subtract, x)

    def lay(t, h, x):
        return ts(T.Y[:, 32 * h:32 * h + 32], T.JG[:], T.sl[:, 2 * t + h:2 * t + h + 1], T.plk[:, h:h + 1], A.add, A.min, x)

    def number(t):
        for h in range(2):
            c = 2 * t + h
            tnum[t + 1] = ts(T.num[:, c + 2:c + 3], T.sl[:, c:c + 1], float(2 * P - 2 * K * t), T.num[:, c:c + 1], A.add, A.min)

    def merge_codes(t, a, n):
        hc[a // 128] = pick(hold(t + 1)[0], hold(t + 1)[1] + a, n, "M%d" % t, T.mrg[:, 16 * t + a // 16:16 * t + (a + n) // 16], arr[t][0], held(t), tm)

    def merge_scales(t, a, n):
        hs[a // 128] = picks(hold(t + 1)[0], hold(t + 1)[1] + a, n, "M%d" % t, T.mrg[:, 16 * t + a // 16:16 * t + (a + n) // 16], arr[t][1], held(t), tm)

    score(0, 1)
    tcon = ts(T.JG[:], T.JG[:], -FAR, None, A.add, None, ta)
    query_codes(1)
    use(0, 0)
    tw = quantize("wk", 0, 128 * O, T.win, ("ldw", 16))
    query_codes(2)
    use(0, 1)

    for t in range(R):
        H, M, u = "H%d" % t, "M%d" % t, t * P
        last, listed = t == R - 1, t % 2 == 0
        if t == 0:
            lay_beside(M, K, H, 0, P, "cp%d" % t, hc[1], hs[1])
        uses = [T.uc[:, h:h + 1] if listed else T.UT[:, 32 * h:32 * h + 1] for h in range(2)]
        z, x = [], []
        for h in range(2):
            mine, other = T.U[:, u + 128 * h:u + 128 * h + 128], T.U[:, u + 128 - 128 * h:u + P - 128 * h]
            ready = tu if t else tu[h:h + 1]
            wait("s", tv[h], *ready)
            z.append(done("s", act.activation(T.sgn[:, 128 * h:128 * h + 128], mine, F.Sign, bias=uses[h], scale=-1.0, accum_out=T.sa[:, h:h + 1])))
            ts(T.X[:, P * h:P * h + 128], mine, uses[h], None, A.is_equal, None, tv[h], *ready)
            x.append(ts(T.X[:, P * h + 128:P * h + P], other, uses[h], -2.0, (A.is_lt, A.is_le)[h], A.mult, tu[1 - h]))
        to = [scan(T.SO[:, P * h:P * h + P], T.G[:], T.X[:, P * h:P * h + P], T.sa[:, h:h + 1], A.mult, A.add, x[h], z[h], tk, tcon) for h in range(2)]
        if listed:
            ahead(t + 1, 0)
            if t:
                products(t - 1, tm, [1], lambda: ahead(t + 1, 1))
            else:
                ahead(t + 1, 1)
        else:
            merge_scales(t - 1, 0, 128)
            lay_beside(M, K, H, 0, K if last else 128, "cp%d" % t, hc[0], hs[0])
            if last:
                products(t - 1, tm)
                store()
            merge_scales(t - 1, 128, K)
            merge_scales(t - 1, 128 + K, K)
            if not last:
                products(t - 1, tm, [1], lambda: ahead(t + 1, 0))
        e0 = mark(t, 0, to[0])
        if not listed:
            merge_codes(t - 1, 128, K)
        e1 = mark(t, 1, to[1])
        s1 = ts(T.st[:], T.SO[:, P - 1:2 * P:P], 0.0, STAY, A.is_le, A.mult)
        for h, e in enumerate((e0, e1)):
            for a in range(2):
                x = turn(T.ET[0:64, 1 + 2 * h + a:640:5], T.E[64 * a:64 * a + 64, 128 * h:128 * h + 128], e)
        s1 = slot(t, s1)
        if not listed:
            merge_codes(t - 1, 128 + K, K)
            if not last:
                lay_beside(M, K + 128, H, 128, 128, "cp%d" % t, hc[1], hs[1])
        if t == 0:
            for o in range(O):
                z = mm(T.py[:, 512 * o:512 * o + P], P, "wk", 128 * o, "H0", 0, tw)
                tyw[o] = tyc[o] = func(T.yw[:, o * W + K:o * W + W], T.py[:, 512 * o:512 * o + P], F.Copy, z)
        x = scan(T.ES[0:32, :], T.ET[0:32, :], T.ET[32:64, :], 0.0, A.max, A.add, x)
        lst = T.lst[:, 4 * t:4 * t + 4]
        tl = [shift(q, T.lst[32 * a:32 * a + 32, 4 * t:4 * t + 4], T.ES[0:32, 159:640:160], 0.5, float((K * t if listed else 0) - P), x) for a, q in enumerate("vvvs")]
        lay(t, 0, s1)
        s1 = lay(t, 1, s1)
        if listed:
            send(T["L%d" % t][:], lst, "arl", t, *tl)
            n = P + K * t
            if t:
                x = mm(T.pa[:, 0:n], n, "qr", 128 * (t + 1), "F%d" % t, 0, trc[t + 1], trs[t + 1], tsqa, *far[t])
                tsqa = tsqf = func(T.sqf[:, 0:n], T.pa[:, 0:n], F.Square, x)
                products(t - 1, tm, [0])
            else:
                for h, bank in enumerate((T.pr[:, 512:640], T.pa[:, 0:128])):
                    x = mm(bank, 128, "qr", 128, "F0", 128 * h, trc[1], trs[1], far[0][1], far[0][2 - 2 * h], tsq[1])
                    tsqa = tsqf = func(T.sqf[:, 128 * h:128 * h + 128], bank, F.Square, x)
                tsq[1] = tsqf
        else:
            S = "S%d" % t
            send_columns(M, S, K, t, (pick(S, 0, K, H, lst, *tl),), (picks(S, 0, K, H, lst, hs[1], *tl),))
            if not last:
                ahead(t + 1, 1)
                products(t - 1, tm, [0])
        if t + 2 < R:
            query_scales(t + 2)
        todo = [] if last else [0, 1]

        def carry():
            if todo:
                h = todo.pop(0)
                a = 128 * h
                out = T.US[:, K + a:K + a + 128] if listed else T.U[:, u + P + a:u + P + a + 128]
                return tt(out, T.U[:, u + a:u + a + 128], T.sqn[:, a:a + 128], A.add, tsn[h], *tu)
            return tadd

        if listed:
            carry()
        x = turn(T.YT[:], T.Y[:], s1)
        tadd = carry()
        x = scan(T.YS[:], T.YR[:], T.YT[:], 0.0, A.add, A.max, x)
        if listed:
            if t + 2 < R:
                number(t)
        elif not last:
            keep(0, uses[0])
            tus = keep(1, uses[1])
        for a in range(4):
            z = copy(T.yb[0:32, :, 2 * a:2 * a + 2], T.YS[32 * a:32 * a + 32, 15:64:16], x)
        if listed:
            town = ts(T.own[:], T.YS[:, 15:64:16], 0.5, float(K), A.mult, A.add)
        tadd = carry()
        for a in range(4):
            tm = ts(T.mrg[32 * a:32 * a + 32, 16 * t:16 * t + 16], T.yb[0:32, :, :], 0.5, float(K), A.mult, A.add, z)
        if listed:
            z, L = came("arl", t), T["L%d" % t][:]
            store(z)
            x = copy(T.US[:, 0:K], T.sqf[:, 0:n].indirect(L), z, tsqf)
            arr[t] = (pick(M, 0, K, "F%d" % t, L), None)
            y = copy(T.UD[:], T.US[:].indirect(T.own[:]), x, town)
            tu = [copy(T.U[:, u + P:u + P + K], T.US[:].indirect(T.mrg[:, 16 * t:16 * t + 4]), tm),
                  func(T.U[:, u + P + K:u + 2 * P], T.US[:].indirect(T.mrg[:, 16 * t + 4:16 * t + 16]), F.Copy, x, tm)]
            arr[t] = (arr[t][0], picks(M, 0, K, "F%d" % t, L, z, *far[t]))
            tv = [turn(T.UT[:], T.UD[:], y)] * 2
            merge_codes(t, 0, 128)
            if t == 0:
                lay_beside("N2", K, "M0", 0, W, "cpn", held(0), *arr[0])
        elif not last:
            N, nxt = "F%d" % (t + 1), t + 1
            left = ("H0", T.lst[:, 0:4]) if t == 1 else ("N2", T.lst[:, 8:12], ("cpn", 64))
            x = pick(N, K, K, *left)
            for i in range(t + 2, min(t + 4, R)):
                query_codes(i)
            ac, as_ = arr[t]
            send_columns(N, M, K, nxt, (ac,), (ac, as_))
            lay_beside(N, 2 * K, "F%d" % (t - 1), 0, P + K * (t - 1), "cpf%d" % nxt, ac, as_, *far[t - 1])
            store()
            if t == 1:
                lay_beside("N2", 0, "M1", 0, K, "cpn")
            z = mm(T.pa[:, 0:128], 128, "qr", 128 * (t + 1), M, 0, ac, as_, held(t), trc[t + 1], trs[t + 1], tsqa)
            for h in range(2):
                merge_codes(t, 128 * h, 128)
                merge_scales(t, 128 * h, 128)
                score(t + 1, h)
            tsqa = func(T.US[:, 0:K], T.pa[:, 0:K], F.Square, z, *tu)
            far[nxt] = (came("arc", nxt), came("ars", nxt), ("cpf%d" % nxt, 32), x, picks(N, K, K, *left))
            tu = [copy(T.U[:, u + P:u + 2 * P].indirect(lst), T.US[:, 0:K], tadd, tsqa)] * 2
            use(t + 1, 0)
            use(t + 1, 1)
            number(t)
        else:
            products(t, tm)
            store()

    for q in ("v", "s", "p", "g"):
        wait("y", (own[q], count[q]))
    wait("y", ("sty", 16 * (R - 1) * O), ("end", 16 * O))
    wait("g", ("loc", sent[0]))
